import numpy as np
import ml_dtypes


def mxq(x, axis, fmt="e4m3"):
    dtype, down = {"e4m3": (ml_dtypes.float8_e4m3fn, 7), "e5m2": (ml_dtypes.float8_e5m2, 14)}[fmt]
    v = np.moveaxis(np.asarray(x, np.float32).astype(ml_dtypes.bfloat16).astype(np.float64), axis, -1)
    blocks = v.reshape(v.shape[:-1] + (-1, 32))
    amax = np.abs(blocks).max(-1, keepdims=True)
    byte = np.maximum(np.where(amax > 0, np.frexp(amax)[1] - 1 + 127, 0) - down, 1)
    scale = np.exp2(byte - 127.0)
    codes = (blocks / scale).astype(np.float32).astype(dtype).astype(np.float64)
    return np.moveaxis((codes * scale).reshape(v.shape), -1, axis)


WIDE = False


def mx_kscale(k):
    if not WIDE:
        return np.ones(k)
    levels = np.array([10, -10, 5, -5, 0])
    if k % 512:
        return np.exp2(np.random.permutation(np.resize(levels, k // 32))).repeat(32)
    a = np.empty((k // 512, 16))
    for p in range(k // 512):
        a[p, :8] = np.random.permutation(np.resize(levels, 8))
        for g in range(8):
            far = levels[np.abs(levels - a[p, g]) >= 10]
            a[p, g + 8] = far[np.random.randint(len(far))]
    return np.exp2(a.ravel()).repeat(32)


def f64(x):
    return np.asarray(x).astype(np.float64)


def striped(idx):
    return np.tile(idx.reshape(-1, 16).T, (8, 1)).astype(np.uint16)


def unstriped(offs):
    return offs[:16].T.reshape(-1).astype(np.int64)


def striped8(idx):
    return np.concatenate([x.reshape(-1, 16).T for x in idx]).astype(np.uint16)


def runs(offs, k):
    lists = np.stack([offs[16 * r : 16 * r + 16].T.reshape(-1) for r in range(8)]).astype(np.int64)
    return lists[np.arange(k) % 512 // 64]


def pack_weight(w):
    k, n = w.shape
    w = f64(np.asarray(w, np.float32).astype(ml_dtypes.bfloat16)).reshape(k // 32, 32, n)
    amax = np.abs(w).max(1)
    byte = np.clip(np.where(amax > 0, np.frexp(amax)[1] - 1 + 127 - 7, 1), 1, 254)
    scaled = (w * np.exp2(127.0 - byte)[:, None, :]).reshape(k, n).astype(np.float32)
    words = np.ascontiguousarray(scaled.reshape(k // 512, 128, 4, n).transpose(0, 1, 3, 2)).astype(ml_dtypes.float8_e4m3fn).view(np.uint8)
    return words, np.ascontiguousarray(byte.astype(np.uint8).reshape(k // 512, 16, n))


def unpack_weight(words, scales):
    g, p, n, _ = words.shape
    vals = np.ascontiguousarray(words).view(ml_dtypes.float8_e4m3fn).astype(np.float64) * np.repeat(np.exp2(scales.astype(np.float64) - 127.0), 8, axis=1)[..., None]
    return vals.transpose(0, 1, 3, 2).reshape(g * 512, n)


def relu(v):
    return np.maximum(v, 0.0)


K, T, S, N, G, H = 512, 2048, 512, 512, 2048, 512


def setup_inputs():
    n = np.random.standard_normal
    s = mx_kscale(K)[:, None]
    u = mx_kscale(H)
    packed_xT = pack_weight(n((K, T)) * s)
    packed_dT = pack_weight(n((K, G)) / s)
    return {
        "x_words": packed_xT[0],
        "x_scales": packed_xT[1],
        "d_words": packed_dT[0],
        "d_scales": packed_dT[1],
        "gn": (np.random.uniform(0.5, 1.5, (H, 1)) * u[:, None]).astype(np.float32),
        "w1": (n((H, N)) / np.sqrt(H) / u[:, None]).astype(np.float32),
        "offs": striped(np.random.permutation(T)[:S]),
        "k1": striped8(np.random.randint(0, G, (8, H))),
        "k2": striped8(np.random.randint(0, G, (8, H))),
    }


def reference(x_words, x_scales, d_words, d_scales, gn, w1, offs, k1, k2):
    d_k1 = unpack_weight(d_words, d_scales)[np.arange(K)[:, None], runs(k1, K)]
    xq = unpack_weight(x_words, x_scales)[:, unstriped(offs)]
    a = 0.0625 * (d_k1.T @ xq)
    d_k2 = unpack_weight(d_words, d_scales)[np.arange(K)[:, None], runs(k2, K)]
    b = 0.0625 * (d_k2.T @ xq)
    z = f64(gn) * (relu(np.maximum(a, b)))
    return mxq(f64(w1), 0, "e4m3").T @ mxq(z, 0, "e4m3")

@@ -1,0 +1,190 @@
+from contextlib import ExitStack
+
+import concourse.mybir as mybir
+
+F32 = mybir.dt.float32
+BF16 = mybir.dt.bfloat16
+I32 = mybir.dt.int32
+U32 = mybir.dt.uint32
+U16 = mybir.dt.uint16
+U8 = mybir.dt.uint8
+FP8X4 = mybir.dt.float8_e4m3fn_x4
+ALU = mybir.AluOpType
+ACT = mybir.ActivationFunctionType
+
+P = 128
+K, T, S, N, G, H = 512, 2048, 512, 512, 2048, 512
+SLOTS = 4
+HALF = S // 2
+SCORE_SCALE = 0.0625
+FLOPS = 2 * K * H * S * 2 + 2 * H * N * S
+
+
+def tile_picked_maxsim_relu_p_kernel(tc, x_words, x_scales, d_words, d_scales, gn, w1, offs, k1, k2, out):
+    nc = tc.nc
+    with ExitStack() as ctx:
+        sb = ctx.enter_context(tc.tile_pool(name="sb", bufs=1))
+        ps = ctx.enter_context(tc.psum_pool(name="ps", bufs=1))
+
+        def tile(shape, dtype, name):
+            return sb.tile(shape, dtype, name=name, align_bytes=64)
+
+        k1_sb = tile([P, H // 16], U16, "k1_sb")
+        k2_sb = tile([P, H // 16], U16, "k2_sb")
+        offs_sb = tile([P, S // 16], U16, "offs_sb")
+        d_scale_tab = tile([P, G], U8, "d_scale_tab")
+        x_scale_tab = tile([P, T], U8, "x_scale_tab")
+        d_word_tab = tile([P, G], U32, "d_word_tab")
+        x_word_tab = tile([P, T], U32, "x_word_tab")
+        gn_pad = tile([P, SLOTS, 8], F32, "gn_pad")
+        w_raw = [tile([P, N], F32, "w_raw%d" % t) for t in range(SLOTS)]
+
+        def load_scale_rows(tab, scales):
+            nc.sync.dma_start(
+                tab[:].bitcast(I32), scales[0].bitcast(I32).unsqueeze(1).to_broadcast([16, 8, scales.shape[2] // 4])
+            )
+
+        def load_words(tab, words):
+            nc.sync.dma_start(tab[:].bitcast(I32), words[0].rearrange("p n t -> p (n t)").bitcast(I32))
+
+        load_scale_rows(d_scale_tab, d_scales)
+        nc.sync.dma_start(k1_sb[:], k1)
+        nc.sync.dma_start(k2_sb[:], k2)
+        load_scale_rows(x_scale_tab, x_scales)
+        nc.sync.dma_start(offs_sb[:], offs)
+        load_words(d_word_tab, d_words)
+        w_rows = w1.rearrange("(b t r) m -> t b r m", t=SLOTS, r=8)
+        for t in range(SLOTS):
+            nc.sync.dma_start(w_raw[t][:], w_rows[t])
+        load_words(x_word_tab, x_words)
+        gn_rows = gn.rearrange("(b t r) o -> t b r o", t=SLOTS, r=8)
+        for t in range(SLOTS):
+            nc.gpsimd.dma_start(gn_pad[:, t, 0:1], gn_rows[t])
+        gn_sb = gn_pad[:, :, 0]
+
+        planes = tile([P, 2 * H + S], U8, "planes")
+        nc.vector.memset(planes[:].bitcast(I32), 0)
+
+        g_abs = tile([P, SLOTS], F32, "g_abs")
+        g_step = tile([P, SLOTS], F32, "g_step")
+        g_sign = tile([P, SLOTS], F32, "g_sign")
+        nc.scalar.activation(g_abs[:], gn_sb, ACT.Abs, scale=SCORE_SCALE)
+        nc.gpsimd.tensor_scalar(g_step[:], gn_sb, 0.0, 2.0, ALU.is_ge, ALU.mult)
+        nc.gpsimd.tensor_scalar(g_sign[:], g_step[:], 1.0, -1.0, ALU.mult, ALU.add)
+
+        d_scale_got = tile([P, 2 * H], U8, "d_scale_got")
+        x_scale_got = tile([P, S], U8, "x_scale_got")
+        scale_dealt = tile([P, 2 * H + S], U8, "scale_dealt")
+        nc.vector.tensor_copy(d_scale_got[:, 0:H], d_scale_tab[:].indirect(k1_sb[:]))
+        nc.vector.tensor_copy(d_scale_got[:, H : 2 * H], d_scale_tab[:].indirect(k2_sb[:]))
+        nc.vector.tensor_copy(x_scale_got[:], x_scale_tab[:].indirect(offs_sb[:]))
+        nc.vector.tensor_copy(
+            scale_dealt[:, 0 : 2 * H].bitcast(I32).rearrange("p (l t b w) -> p l t b w", l=2, t=SLOTS, w=2),
+            d_scale_got[:].bitcast(I32).rearrange("p (l b t w) -> p l t b w", l=2, t=SLOTS, w=2),
+        )
+        nc.vector.tensor_copy(scale_dealt[:, 2 * H :].bitcast(I32), x_scale_got[:].bitcast(I32))
+        for r in range(4):
+            nc.sync.dma_start(planes[:].bitcast(I32)[r:P:32, :], scale_dealt[:].bitcast(I32)[8 * r : P : 32, :])
+
+        d_codes = []
+        for name, lst in (("a", k1_sb), ("b", k2_sb)):
+            got = tile([P, H], U32, "d_word_got_" + name)
+            dealt = tile([P, H], U32, "d_codes_" + name)
+            nc.vector.tensor_copy(got[:], d_word_tab[:].indirect(lst[:]))
+            nc.vector.tensor_copy(
+                dealt[:].bitcast(I32).rearrange("p (t b r) -> p t b r", t=SLOTS, r=8),
+                got[:].bitcast(I32).rearrange("p (b t r) -> p t b r", t=SLOTS, r=8),
+            )
+            d_codes.append(dealt)
+
+        w_signed = tile([P, SLOTS, N], BF16, "w_signed")
+        w_woven = tile([P, N * SLOTS], BF16, "w_woven")
+        for t in range(SLOTS):
+            nc.scalar.activation(w_signed[:, t, :], w_raw[t][:], ACT.Copy, scale=g_sign[:, t : t + 1])
+        nc.scalar.copy(
+            w_woven[:].rearrange("p (c i t) -> p c t i", i=4, t=SLOTS),
+            w_signed[:].rearrange("p t (c i) -> p c t i", i=4),
+        )
+
+        x_codes = []
+        for h in range(2):
+            got = tile([P, HALF], U32, "x_codes%d" % h)
+            nc.vector.tensor_copy(got[:], x_word_tab[:].indirect(offs_sb[:, 16 * h : 16 * (h + 1)]))
+            x_codes.append(got)
+
+        w_codes = tile([P, N], U32, "w_codes")
+        w_plane = tile([P, N], U8, "w_plane")
+        nc.vector.quantize_mx(out=w_codes[:].bitcast(FP8X4), scales=w_plane[:], in_=w_woven[:])
+
+        def scores(h):
+            banks = {}
+            for pair in range(2):
+                for side in range(2):
+                    bank = ps.tile([P, 2, HALF], F32, name="bank%d%d%d" % (h, pair, side))
+                    for u in range(2):
+                        t = 2 * pair + u
+                        nc.tensor.matmul_mx(
+                            out=bank[:, u, :],
+                            lhsT=d_codes[side][:, P * t : P * (t + 1)].bitcast(FP8X4),
+                            lhsT_scale=planes[:, side * H + P * t : side * H + P * (t + 1)],
+                            rhs=x_codes[h][:].bitcast(FP8X4),
+                            rhs_scale=planes[:, 2 * H + HALF * h : 2 * H + HALF * (h + 1)],
+                            start=True,
+                            stop=True,
+                        )
+                    banks[pair, side] = bank
+            return banks
+
+        def best(h, banks, z, t):
+            ra = tile([P, HALF], F32, "ra%d%d" % (h, t))
+            nc.scalar.activation(ra[:], banks[t // 2, 0][:, t % 2, :], ACT.Relu, scale=g_abs[:, t : t + 1])
+            nc.vector.scalar_tensor_tensor(
+                z[:, t, :], banks[t // 2, 1][:, t % 2, :], g_abs[:, t : t + 1], ra[:], ALU.mult, ALU.max
+            )
+
+        def weave(h, z):
+            woven = tile([P, HALF * SLOTS], BF16, "z_woven%d" % h)
+            nc.vector.tensor_copy(
+                woven[:].rearrange("p (c i t) -> p c t i", i=4, t=SLOTS),
+                z[:].rearrange("p t (c i) -> p c t i", i=4),
+            )
+            return woven
+
+        def quantise(h, woven):
+            codes = tile([P, HALF], U32, "z_codes%d" % h)
+            plane = tile([P, HALF], U8, "z_plane%d" % h)
+            nc.vector.quantize_mx(out=codes[:].bitcast(FP8X4), scales=plane[:], in_=woven[:])
+            return codes, plane
+
+        out_rows = out.rearrange("(v u p) j -> v p u j", u=2, p=P)
+
+        def values(h, codes, plane, copy_engines):
+            for v in range(2):
+                bank = ps.tile([P, 2, HALF], F32, name="bank%d%d%d" % (h, v, 0))
+                for u in range(2):
+                    m0 = P * (2 * v + u)
+                    nc.tensor.matmul_mx(
+                        out=bank[:, u, :],
+                        lhsT=w_codes[:, m0 : m0 + P].bitcast(FP8X4),
+                        lhsT_scale=w_plane[:, m0 : m0 + P],
+                        rhs=codes[:].bitcast(FP8X4),
+                        rhs_scale=plane[:],
+                        start=True,
+                        stop=True,
+                    )
+                res = tile([P, 2, HALF], F32, "res%d%d" % (h, v))
+                copy_engines[v](res[:], bank[:])
+                nc.sync.dma_start(out_rows[v][:, :, HALF * h : HALF * (h + 1)], res[:])
+
+        banks = [scores(0), scores(1)]
+        z = [tile([P, SLOTS, HALF], BF16, "z%d" % h) for h in range(2)]
+        for t in range(SLOTS):
+            best(0, banks[0], z[0], t)
+        woven0 = weave(0, z[0])
+        best(1, banks[1], z[1], 0)
+        q0 = quantise(0, woven0)
+        for t in range(1, SLOTS):
+            best(1, banks[1], z[1], t)
+        values(0, q0[0], q0[1], (nc.scalar.copy, nc.scalar.copy))
+        q1 = quantise(1, weave(1, z[1]))
+        values(1, q1[0], q1[1], (nc.vector.tensor_copy, nc.scalar.copy))

@@ -1,6 +1,7 @@
 from contextlib import ExitStack
 
 import concourse.mybir as mybir
+from concourse.masks import make_identity
 
 F32 = mybir.dt.float32
 BF16 = mybir.dt.bfloat16
@@ -36,7 +37,8 @@ def tile_picked_maxsim_relu_p_kernel(tc, x_words, x_scales, d_words, d_scales, g
         x_scale_tab = tile([P, T], U8, "x_scale_tab")
         d_word_tab = tile([P, G], U32, "d_word_tab")
         x_word_tab = tile([P, T], U32, "x_word_tab")
-        gn_pad = tile([P, SLOTS, 8], F32, "gn_pad")
+        gn_rows = tile([P, P], F32, "gn_rows")
+        identity = tile([P, P], F32, "identity")
         w_raw = [tile([P, N], F32, "w_raw%d" % t) for t in range(SLOTS)]
 
         def load_scale_rows(tab, scales):
@@ -50,17 +52,20 @@ def tile_picked_maxsim_relu_p_kernel(tc, x_words, x_scales, d_words, d_scales, g
         load_scale_rows(d_scale_tab, d_scales)
         nc.sync.dma_start(k1_sb[:], k1)
         nc.sync.dma_start(k2_sb[:], k2)
-        load_scale_rows(x_scale_tab, x_scales)
         nc.sync.dma_start(offs_sb[:], offs)
+        nc.vector.memset(x_scale_tab[:].bitcast(I32), 0)
+        nc.sync.dma_start(x_scale_tab[:].bitcast(I32)[0:P:8, :], x_scales[0].bitcast(I32))
         load_words(d_word_tab, d_words)
         w_rows = w1.rearrange("(b t r) m -> t b r m", t=SLOTS, r=8)
         for t in range(SLOTS):
             nc.sync.dma_start(w_raw[t][:], w_rows[t])
         load_words(x_word_tab, x_words)
-        gn_rows = gn.rearrange("(b t r) o -> t b r o", t=SLOTS, r=8)
-        for t in range(SLOTS):
-            nc.gpsimd.dma_start(gn_pad[:, t, 0:1], gn_rows[t])
-        gn_sb = gn_pad[:, :, 0]
+        nc.gpsimd.memset(gn_rows[:], 0.0)
+        nc.scalar.dma_start(gn_rows[0:SLOTS, :], gn.rearrange("(b t r) o -> t b (r o)", t=SLOTS, r=8))
+        make_identity(nc, identity[:])
+        gn_bank = ps.tile([P, 2, HALF], F32, name="bank111")
+        nc.tensor.transpose(gn_bank[:, 0, 0:P], gn_rows[:], identity[:])
+        gn_sb = gn_bank[:, 0, 0:SLOTS]
 
         planes = tile([P, 2 * H + S], U8, "planes")
         nc.vector.memset(planes[:].bitcast(I32), 0)
@@ -68,9 +73,9 @@ def tile_picked_maxsim_relu_p_kernel(tc, x_words, x_scales, d_words, d_scales, g
         g_abs = tile([P, SLOTS], F32, "g_abs")
         g_step = tile([P, SLOTS], F32, "g_step")
         g_sign = tile([P, SLOTS], F32, "g_sign")
+        nc.scalar.activation(g_step[:], gn_sb, ACT.Sign)
         nc.scalar.activation(g_abs[:], gn_sb, ACT.Abs, scale=SCORE_SCALE)
-        nc.gpsimd.tensor_scalar(g_step[:], gn_sb, 0.0, 2.0, ALU.is_ge, ALU.mult)
-        nc.gpsimd.tensor_scalar(g_sign[:], g_step[:], 1.0, -1.0, ALU.mult, ALU.add)
+        nc.scalar.activation(g_sign[:], g_step[:], ACT.Sign, bias=0.5)
 
         d_scale_got = tile([P, 2 * H], U8, "d_scale_got")
         x_scale_got = tile([P, S], U8, "x_scale_got")
@@ -87,6 +92,7 @@ def tile_picked_maxsim_relu_p_kernel(tc, x_words, x_scales, d_words, d_scales, g
             nc.sync.dma_start(planes[:].bitcast(I32)[r:P:32, :], scale_dealt[:].bitcast(I32)[8 * r : P : 32, :])
 
         d_codes = []
+        d_got = []
         for name, lst in (("a", k1_sb), ("b", k2_sb)):
             got = tile([P, H], U32, "d_word_got_" + name)
             dealt = tile([P, H], U32, "d_codes_" + name)
@@ -96,6 +102,19 @@ def tile_picked_maxsim_relu_p_kernel(tc, x_words, x_scales, d_words, d_scales, g
                 got[:].bitcast(I32).rearrange("p (b t r) -> p t b r", t=SLOTS, r=8),
             )
             d_codes.append(dealt)
+            d_got.append(got)
+
+        warm = ps.tile([P, 2, HALF], F32, name="bank111")
+        for t in range(3):
+            nc.tensor.matmul_mx(
+                out=warm[:].rearrange("p u j -> p (u j)"),
+                lhsT=d_got[min(t, 1)][:, P * t : P * (t + 1)].bitcast(FP8X4),
+                lhsT_scale=scale_dealt[:, P * t : P * (t + 1)],
+                rhs=d_got[0][:].bitcast(FP8X4),
+                rhs_scale=scale_dealt[:, 0:H],
+                start=True,
+                stop=True,
+            )
 
         w_signed = tile([P, SLOTS, N], BF16, "w_signed")
         w_woven = tile([P, N * SLOTS], BF16, "w_woven")
@@ -144,10 +163,20 @@ def tile_picked_maxsim_relu_p_kernel(tc, x_words, x_scales, d_words, d_scales, g
 
         def weave(h, z):
             woven = tile([P, HALF * SLOTS], BF16, "z_woven%d" % h)
-            nc.vector.tensor_copy(
-                woven[:].rearrange("p (c i t) -> p c t i", i=4, t=SLOTS),
-                z[:].rearrange("p t (c i) -> p c t i", i=4),
-            )
+            if h == 0:
+                nc.gpsimd.tensor_scalar(
+                    woven[:].rearrange("p (c t) -> p c t", t=SLOTS),
+                    z[:].rearrange("p t c -> p c t"),
+                    1.0,
+                    0.0,
+                    ALU.mult,
+                    ALU.add,
+                )
+            else:
+                dst = woven[:].rearrange("p (c i t) -> p c t i", i=4, t=SLOTS)
+                src = z[:].rearrange("p t (c i) -> p c t i", i=4)
+                nc.vector.tensor_copy(dst[:, 0:44], src[:, 0:44])
+                nc.scalar.copy(dst[:, 44:64], src[:, 44:64])
             return woven
 
         def quantise(h, woven):
@@ -156,13 +185,13 @@ def tile_picked_maxsim_relu_p_kernel(tc, x_words, x_scales, d_words, d_scales, g
             nc.vector.quantize_mx(out=codes[:].bitcast(FP8X4), scales=plane[:], in_=woven[:])
             return codes, plane
 
-        out_rows = out.rearrange("(v u p) j -> v p u j", u=2, p=P)
-
-        def values(h, codes, plane, copy_engines):
-            for v in range(2):
-                bank = ps.tile([P, 2, HALF], F32, name="bank%d%d%d" % (h, v, 0))
-                for u in range(2):
-                    m0 = P * (2 * v + u)
+        def values(h, codes, plane, bank_names, copy_engines):
+            group = SLOTS // len(bank_names)
+            out_rows = out.rearrange("(v u p) j -> v p u j", u=group, p=P)
+            for v, bank_name in enumerate(bank_names):
+                bank = ps.tile([P, group, HALF], F32, name=bank_name)
+                for u in range(group):
+                    m0 = P * (group * v + u)
                     nc.tensor.matmul_mx(
                         out=bank[:, u, :],
                         lhsT=w_codes[:, m0 : m0 + P].bitcast(FP8X4),
@@ -172,7 +201,7 @@ def tile_picked_maxsim_relu_p_kernel(tc, x_words, x_scales, d_words, d_scales, g
                         start=True,
                         stop=True,
                     )
-                res = tile([P, 2, HALF], F32, "res%d%d" % (h, v))
+                res = tile([P, group, HALF], F32, "res%d%d" % (h, v))
                 copy_engines[v](res[:], bank[:])
                 nc.sync.dma_start(out_rows[v][:, :, HALF * h : HALF * (h + 1)], res[:])
 
@@ -181,10 +210,15 @@ def tile_picked_maxsim_relu_p_kernel(tc, x_words, x_scales, d_words, d_scales, g
         for t in range(SLOTS):
             best(0, banks[0], z[0], t)
         woven0 = weave(0, z[0])
-        best(1, banks[1], z[1], 0)
-        q0 = quantise(0, woven0)
-        for t in range(1, SLOTS):
+        for t in range(SLOTS):
             best(1, banks[1], z[1], t)
-        values(0, q0[0], q0[1], (nc.scalar.copy, nc.scalar.copy))
+        q0 = quantise(0, woven0)
+        values(0, q0[0], q0[1], ("bank000", "bank010"), (nc.scalar.copy, nc.scalar.copy))
         q1 = quantise(1, weave(1, z[1]))
-        values(1, q1[0], q1[1], (nc.vector.tensor_copy, nc.scalar.copy))
+        values(
+            1,
+            q1[0],
+            q1[1],
+            ("bank100", "bank110", "bank101", "bank111"),
+            (nc.vector.tensor_copy, nc.scalar.copy, nc.vector.tensor_copy, nc.scalar.copy),
+        )

@@ -42,19 +42,19 @@ def tile_picked_maxsim_relu_p_kernel(tc, x_words, x_scales, d_words, d_scales, g
         w_raw = [tile([P, N], F32, "w_raw%d" % t) for t in range(SLOTS)]
 
         def load_scale_rows(tab, scales):
-            nc.sync.dma_start(
-                tab[:].bitcast(I32), scales[0].bitcast(I32).unsqueeze(1).to_broadcast([16, 8, scales.shape[2] // 4])
-            )
+            nc.sync.dma_start(tab[:].bitcast(I32)[0:P:8, :], scales[0].bitcast(I32))
 
         def load_words(tab, words):
             nc.sync.dma_start(tab[:].bitcast(I32), words[0].rearrange("p n t -> p (n t)").bitcast(I32))
 
-        load_scale_rows(d_scale_tab, d_scales)
+        nc.gpsimd.memset(d_scale_tab[:, 0 : G // 2].bitcast(I32), 0)
+        nc.vector.memset(d_scale_tab[:, G // 2 :].bitcast(I32), 0)
+        nc.vector.memset(x_scale_tab[:].bitcast(I32), 0)
         nc.sync.dma_start(k1_sb[:], k1)
+        load_scale_rows(d_scale_tab, d_scales)
         nc.sync.dma_start(k2_sb[:], k2)
         nc.sync.dma_start(offs_sb[:], offs)
-        nc.vector.memset(x_scale_tab[:].bitcast(I32), 0)
-        nc.sync.dma_start(x_scale_tab[:].bitcast(I32)[0:P:8, :], x_scales[0].bitcast(I32))
+        load_scale_rows(x_scale_tab, x_scales)
         load_words(d_word_tab, d_words)
         w_rows = w1.rearrange("(b t r) m -> t b r m", t=SLOTS, r=8)
         for t in range(SLOTS):
@@ -163,20 +163,9 @@ def tile_picked_maxsim_relu_p_kernel(tc, x_words, x_scales, d_words, d_scales, g
 
         def weave(h, z):
             woven = tile([P, HALF * SLOTS], BF16, "z_woven%d" % h)
-            if h == 0:
-                nc.gpsimd.tensor_scalar(
-                    woven[:].rearrange("p (c t) -> p c t", t=SLOTS),
-                    z[:].rearrange("p t c -> p c t"),
-                    1.0,
-                    0.0,
-                    ALU.mult,
-                    ALU.add,
-                )
-            else:
-                dst = woven[:].rearrange("p (c i t) -> p c t i", i=4, t=SLOTS)
-                src = z[:].rearrange("p t (c i) -> p c t i", i=4)
-                nc.vector.tensor_copy(dst[:, 0:44], src[:, 0:44])
-                nc.scalar.copy(dst[:, 44:64], src[:, 44:64])
+            dst = woven[:].rearrange("p (c i t) -> p c t i", i=4, t=SLOTS)
+            src = z[:].rearrange("p t (c i) -> p c t i", i=4)
+            (nc.scalar.copy, nc.vector.tensor_copy)[h](dst, src)
             return woven
 
         def quantise(h, woven):
@@ -207,18 +196,15 @@ def tile_picked_maxsim_relu_p_kernel(tc, x_words, x_scales, d_words, d_scales, g
 
         banks = [scores(0), scores(1)]
         z = [tile([P, SLOTS, HALF], BF16, "z%d" % h) for h in range(2)]
-        for t in range(SLOTS):
-            best(0, banks[0], z[0], t)
-        woven0 = weave(0, z[0])
-        for t in range(SLOTS):
-            best(1, banks[1], z[1], t)
-        q0 = quantise(0, woven0)
-        values(0, q0[0], q0[1], ("bank000", "bank010"), (nc.scalar.copy, nc.scalar.copy))
-        q1 = quantise(1, weave(1, z[1]))
-        values(
-            1,
-            q1[0],
-            q1[1],
-            ("bank100", "bank110", "bank101", "bank111"),
-            (nc.vector.tensor_copy, nc.scalar.copy, nc.vector.tensor_copy, nc.scalar.copy),
-        )
+        for h in range(2):
+            for t in range(SLOTS):
+                best(h, banks[h], z[h], t)
+        woven = [weave(h, z[h]) for h in range(2)]
+        quantised = {h: quantise(h, woven[h]) for h in (0, 1)}
+        for h in (0, 1):
+            values(
+                h,
+                *quantised[h],
+                ["bank%d%d%d" % (h, pair, side) for side in range(2) for pair in range(2)],
+                (nc.scalar.copy, nc.vector.tensor_copy, nc.scalar.copy, nc.vector.tensor_copy),
+            )

@@ -41,8 +41,8 @@ def tile_picked_maxsim_relu_p_kernel(tc, x_words, x_scales, d_words, d_scales, g
         identity = tile([P, P], F32, "identity")
         w_raw = [tile([P, N], F32, "w_raw%d" % t) for t in range(SLOTS)]
 
-        def load_scale_rows(tab, scales):
-            nc.sync.dma_start(tab[:].bitcast(I32)[0:P:8, :], scales[0].bitcast(I32))
+        def load_scale_rows(queue, tab, scales):
+            queue.dma_start(tab[:].bitcast(I32)[0:P:8, :], scales[0].bitcast(I32))
 
         def load_words(tab, words):
             nc.sync.dma_start(tab[:].bitcast(I32), words[0].rearrange("p n t -> p (n t)").bitcast(I32))
@@ -51,10 +51,10 @@ def tile_picked_maxsim_relu_p_kernel(tc, x_words, x_scales, d_words, d_scales, g
         nc.vector.memset(d_scale_tab[:, G // 2 :].bitcast(I32), 0)
         nc.vector.memset(x_scale_tab[:].bitcast(I32), 0)
         nc.sync.dma_start(k1_sb[:], k1)
-        load_scale_rows(d_scale_tab, d_scales)
+        load_scale_rows(nc.sync, d_scale_tab, d_scales)
         nc.sync.dma_start(k2_sb[:], k2)
         nc.sync.dma_start(offs_sb[:], offs)
-        load_scale_rows(x_scale_tab, x_scales)
+        load_scale_rows(nc.sync, x_scale_tab, x_scales)
         load_words(d_word_tab, d_words)
         w_rows = w1.rearrange("(b t r) m -> t b r m", t=SLOTS, r=8)
         for t in range(SLOTS):
@@ -165,7 +165,7 @@ def tile_picked_maxsim_relu_p_kernel(tc, x_words, x_scales, d_words, d_scales, g
             woven = tile([P, HALF * SLOTS], BF16, "z_woven%d" % h)
             dst = woven[:].rearrange("p (c i t) -> p c t i", i=4, t=SLOTS)
             src = z[:].rearrange("p t (c i) -> p c t i", i=4)
-            (nc.scalar.copy, nc.vector.tensor_copy)[h](dst, src)
+            nc.vector.tensor_copy(dst, src)
             return woven
 
         def quantise(h, woven):
@@ -196,15 +196,15 @@ def tile_picked_maxsim_relu_p_kernel(tc, x_words, x_scales, d_words, d_scales, g
 
         banks = [scores(0), scores(1)]
         z = [tile([P, SLOTS, HALF], BF16, "z%d" % h) for h in range(2)]
-        for h in range(2):
-            for t in range(SLOTS):
-                best(h, banks[h], z[h], t)
-        woven = [weave(h, z[h]) for h in range(2)]
-        quantised = {h: quantise(h, woven[h]) for h in (0, 1)}
-        for h in (0, 1):
-            values(
-                h,
-                *quantised[h],
-                ["bank%d%d%d" % (h, pair, side) for side in range(2) for pair in range(2)],
-                (nc.scalar.copy, nc.vector.tensor_copy, nc.scalar.copy, nc.vector.tensor_copy),
-            )
+        names = [["bank%d%d%d" % (h, pair, side) for side in range(2) for pair in range(2)] for h in range(2)]
+        for t in range(SLOTS):
+            best(0, banks[0], z[0], t)
+        woven0 = weave(0, z[0])
+        best(1, banks[1], z[1], 0)
+        q0 = quantise(0, woven0)
+        for t in range(1, SLOTS):
+            best(1, banks[1], z[1], t)
+        values(0, *q0, names[0], (nc.scalar.copy,) * 4)
+        woven1 = weave(1, z[1])
+        q1 = quantise(1, woven1)
+        values(1, *q1, names[1], (nc.scalar.copy, nc.vector.tensor_copy, nc.scalar.copy, nc.vector.tensor_copy))

@@ -49,15 +49,17 @@ def tile_picked_maxsim_relu_p_kernel(tc, x_words, x_scales, d_words, d_scales, g
 
         nc.gpsimd.memset(d_scale_tab[:, 0 : G // 2].bitcast(I32), 0)
         nc.vector.memset(d_scale_tab[:, G // 2 :].bitcast(I32), 0)
-        nc.vector.memset(x_scale_tab[:].bitcast(I32), 0)
+        nc.gpsimd.memset(x_scale_tab[:, 0 : T // 2].bitcast(I32), 0)
+        nc.vector.memset(x_scale_tab[:, T // 2 :].bitcast(I32), 0)
+        w_rows = w1.rearrange("(b t r) m -> t b r m", t=SLOTS, r=8)
+        nc.sync.dma_start(w_raw[0][:], w_rows[0])
         nc.sync.dma_start(k1_sb[:], k1)
         load_scale_rows(nc.sync, d_scale_tab, d_scales)
         nc.sync.dma_start(k2_sb[:], k2)
+        load_words(d_word_tab, d_words)
         nc.sync.dma_start(offs_sb[:], offs)
         load_scale_rows(nc.sync, x_scale_tab, x_scales)
-        load_words(d_word_tab, d_words)
-        w_rows = w1.rearrange("(b t r) m -> t b r m", t=SLOTS, r=8)
-        for t in range(SLOTS):
+        for t in range(1, SLOTS):
             nc.sync.dma_start(w_raw[t][:], w_rows[t])
         load_words(x_word_tab, x_words)
         nc.gpsimd.memset(gn_rows[:], 0.0)
@@ -79,7 +81,7 @@ def tile_picked_maxsim_relu_p_kernel(tc, x_words, x_scales, d_words, d_scales, g
 
         d_scale_got = tile([P, 2 * H], U8, "d_scale_got")
         x_scale_got = tile([P, S], U8, "x_scale_got")
-        scale_dealt = tile([P, 2 * H + S], U8, "scale_dealt")
+        scale_dealt = tile([P, 2 * H + S], U8, "x_scale_tab")
         nc.vector.tensor_copy(d_scale_got[:, 0:H], d_scale_tab[:].indirect(k1_sb[:]))
         nc.vector.tensor_copy(d_scale_got[:, H : 2 * H], d_scale_tab[:].indirect(k2_sb[:]))
         nc.vector.tensor_copy(x_scale_got[:], x_scale_tab[:].indirect(offs_sb[:]))
@@ -91,18 +93,15 @@ def tile_picked_maxsim_relu_p_kernel(tc, x_words, x_scales, d_words, d_scales, g
         for r in range(4):
             nc.sync.dma_start(planes[:].bitcast(I32)[r:P:32, :], scale_dealt[:].bitcast(I32)[8 * r : P : 32, :])
 
-        d_codes = []
-        d_got = []
-        for name, lst in (("a", k1_sb), ("b", k2_sb)):
-            got = tile([P, H], U32, "d_word_got_" + name)
-            dealt = tile([P, H], U32, "d_codes_" + name)
-            nc.vector.tensor_copy(got[:], d_word_tab[:].indirect(lst[:]))
+        d_got = [tile([P, H], U32, name) for name in ("d_scale_got", "x_scale_got")]
+        d_codes = [tile([P, H], U32, "d_codes%d" % side) for side in range(2)]
+        for side, lst in enumerate((k1_sb, k2_sb)):
+            nc.vector.tensor_copy(d_got[side][:], d_word_tab[:].indirect(lst[:]))
+        for side in range(2):
             nc.vector.tensor_copy(
-                dealt[:].bitcast(I32).rearrange("p (t b r) -> p t b r", t=SLOTS, r=8),
-                got[:].bitcast(I32).rearrange("p (b t r) -> p t b r", t=SLOTS, r=8),
+                d_codes[side][:].bitcast(I32).rearrange("p (t b r) -> p t b r", t=SLOTS, r=8),
+                d_got[side][:].bitcast(I32).rearrange("p (b t r) -> p t b r", t=SLOTS, r=8),
             )
-            d_codes.append(dealt)
-            d_got.append(got)
 
         warm = ps.tile([P, 2, HALF], F32, name="bank111")
         for t in range(3):
@@ -131,10 +130,6 @@ def tile_picked_maxsim_relu_p_kernel(tc, x_words, x_scales, d_words, d_scales, g
             nc.vector.tensor_copy(got[:], x_word_tab[:].indirect(offs_sb[:, 16 * h : 16 * (h + 1)]))
             x_codes.append(got)
 
-        w_codes = tile([P, N], U32, "w_codes")
-        w_plane = tile([P, N], U8, "w_plane")
-        nc.vector.quantize_mx(out=w_codes[:].bitcast(FP8X4), scales=w_plane[:], in_=w_woven[:])
-
         def scores(h):
             banks = {}
             for pair in range(2):
@@ -154,31 +149,35 @@ def tile_picked_maxsim_relu_p_kernel(tc, x_words, x_scales, d_words, d_scales, g
                     banks[pair, side] = bank
             return banks
 
-        def best(h, banks, z, t):
-            ra = tile([P, HALF], F32, "ra%d%d" % (h, t))
-            nc.scalar.activation(ra[:], banks[t // 2, 0][:, t % 2, :], ACT.Relu, scale=g_abs[:, t : t + 1])
-            nc.vector.scalar_tensor_tensor(
-                z[:, t, :], banks[t // 2, 1][:, t % 2, :], g_abs[:, t : t + 1], ra[:], ALU.mult, ALU.max
-            )
+        banks = [scores(0), scores(1)]
+        ra = [[tile([P, HALF], F32, "ra%d%d" % (h, t)) for t in range(SLOTS)] for h in range(2)]
 
-        def weave(h, z):
-            woven = tile([P, HALF * SLOTS], BF16, "z_woven%d" % h)
-            dst = woven[:].rearrange("p (c i t) -> p c t i", i=4, t=SLOTS)
-            src = z[:].rearrange("p t (c i) -> p c t i", i=4)
-            nc.vector.tensor_copy(dst, src)
-            return woven
+        def relu_a(h):
+            for t in range(SLOTS):
+                nc.scalar.activation(ra[h][t][:], banks[h][t // 2, 0][:, t % 2, :], ACT.Relu, scale=g_abs[:, t : t + 1])
 
-        def quantise(h, woven):
-            codes = tile([P, HALF], U32, "z_codes%d" % h)
-            plane = tile([P, HALF], U8, "z_plane%d" % h)
+        def best(name, h, lo, width):
+            z = tile([P, SLOTS, width], BF16, "z" + name)
+            for t in range(SLOTS):
+                nc.vector.scalar_tensor_tensor(
+                    z[:, t, :], banks[h][t // 2, 1][:, t % 2, lo : lo + width], g_abs[:, t : t + 1], ra[h][t][:, lo : lo + width], ALU.mult, ALU.max
+                )
+            return z
+
+        def weave(copy, woven, z):
+            copy(woven.rearrange("p (c i t) -> p c t i", i=4, t=SLOTS), z.rearrange("p t (c i) -> p c t i", i=4))
+
+        def quantise(name, woven, width):
+            codes = tile([P, width], U32, "codes" + name)
+            plane = tile([P, width], U8, "plane" + name)
             nc.vector.quantize_mx(out=codes[:].bitcast(FP8X4), scales=plane[:], in_=woven[:])
             return codes, plane
 
-        def values(h, codes, plane, bank_names, copy_engines):
+        def values(name, j0, width, codes, plane, bank_names, copy_engines):
             group = SLOTS // len(bank_names)
             out_rows = out.rearrange("(v u p) j -> v p u j", u=group, p=P)
             for v, bank_name in enumerate(bank_names):
-                bank = ps.tile([P, group, HALF], F32, name=bank_name)
+                bank = ps.tile([P, group, width], F32, name=bank_name)
                 for u in range(group):
                     m0 = P * (group * v + u)
                     nc.tensor.matmul_mx(
@@ -190,21 +189,29 @@ def tile_picked_maxsim_relu_p_kernel(tc, x_words, x_scales, d_words, d_scales, g
                         start=True,
                         stop=True,
                     )
-                res = tile([P, group, HALF], F32, "res%d%d" % (h, v))
+                res = tile([P, group, width], F32, "res%s%d" % (name, v))
                 copy_engines[v](res[:], bank[:])
-                nc.sync.dma_start(out_rows[v][:, :, HALF * h : HALF * (h + 1)], res[:])
+                nc.sync.dma_start(out_rows[v][:, :, j0 : j0 + width], res[:])
 
-        banks = [scores(0), scores(1)]
-        z = [tile([P, SLOTS, HALF], BF16, "z%d" % h) for h in range(2)]
         names = [["bank%d%d%d" % (h, pair, side) for side in range(2) for pair in range(2)] for h in range(2)]
-        for t in range(SLOTS):
-            best(0, banks[0], z[0], t)
-        woven0 = weave(0, z[0])
-        best(1, banks[1], z[1], 0)
-        q0 = quantise(0, woven0)
+        woven = [tile([P, HALF * SLOTS], BF16, "woven%d" % h) for h in range(2)]
+        w_codes, w_plane = quantise("w", w_woven, N)
+        relu_a(0)
+        z0 = best("0", 0, 0, HALF)
+        relu_a(1)
+        weave(nc.vector.tensor_copy, woven[0][:], z0[:])
+        z1 = tile([P, SLOTS, HALF], BF16, "z1")
+
+        def best_slot(t):
+            nc.vector.scalar_tensor_tensor(
+                z1[:, t, :], banks[1][t // 2, 1][:, t % 2, :], g_abs[:, t : t + 1], ra[1][t][:], ALU.mult, ALU.max
+            )
+
+        best_slot(0)
+        q0 = quantise("0", woven[0], HALF)
         for t in range(1, SLOTS):
-            best(1, banks[1], z[1], t)
-        values(0, *q0, names[0], (nc.scalar.copy,) * 4)
-        woven1 = weave(1, z[1])
-        q1 = quantise(1, woven1)
-        values(1, *q1, names[1], (nc.scalar.copy, nc.vector.tensor_copy, nc.scalar.copy, nc.vector.tensor_copy))
+            best_slot(t)
+        values("0", 0, HALF, *q0, names[0], (nc.scalar.copy,) * 4)
+        weave(nc.vector.tensor_copy, woven[1][:], z1[:])
+        q1 = quantise("1", woven[1], HALF)
+        values("1", HALF, HALF, *q1, names[1], (nc.scalar.copy, nc.vector.tensor_copy) * 2)

@@ -27,14 +27,19 @@ def tile_picked_maxsim_relu_p_kernel(tc, x_words, x_scales, d_words, d_scales, g
         sb = ctx.enter_context(tc.tile_pool(name="sb", bufs=1))
         ps = ctx.enter_context(tc.psum_pool(name="ps", bufs=1))
 
+        reuse = ctx.enter_context(tc.tile_pool(name="reuse", bufs=1))
+
         def tile(shape, dtype, name):
             return sb.tile(shape, dtype, name=name, align_bytes=64)
+
+        def tile_at(offset, shape, dtype, name):
+            return reuse.tile(shape, dtype, name=name, align_bytes=64, offset=offset)
 
         k1_sb = tile([P, H // 16], U16, "k1_sb")
         k2_sb = tile([P, H // 16], U16, "k2_sb")
         offs_sb = tile([P, S // 16], U16, "offs_sb")
         d_scale_tab = tile([P, G], U8, "d_scale_tab")
-        x_scale_tab = tile([P, T], U8, "x_scale_tab")
+        x_scale_tab = tile_at(0, [P, T], U8, "x_scale_tab")
         d_word_tab = tile([P, G], U32, "d_word_tab")
         x_word_tab = tile([P, T], U32, "x_word_tab")
         gn_rows = tile([P, P], F32, "gn_rows")
@@ -47,10 +52,9 @@ def tile_picked_maxsim_relu_p_kernel(tc, x_words, x_scales, d_words, d_scales, g
         def load_words(tab, words):
             nc.sync.dma_start(tab[:].bitcast(I32), words[0].rearrange("p n t -> p (n t)").bitcast(I32))
 
-        nc.gpsimd.memset(d_scale_tab[:, 0 : G // 2].bitcast(I32), 0)
-        nc.vector.memset(d_scale_tab[:, G // 2 :].bitcast(I32), 0)
-        nc.gpsimd.memset(x_scale_tab[:, 0 : T // 2].bitcast(I32), 0)
-        nc.vector.memset(x_scale_tab[:, T // 2 :].bitcast(I32), 0)
+        nc.vector.memset(d_scale_tab[:].bitcast(I32), 0)
+        nc.vector.memset(gn_rows[:], 0.0)
+        nc.vector.memset(x_scale_tab[:].bitcast(I32), 0)
         w_rows = w1.rearrange("(b t r) m -> t b r m", t=SLOTS, r=8)
         nc.sync.dma_start(w_raw[0][:], w_rows[0])
         nc.sync.dma_start(k1_sb[:], k1)
@@ -62,15 +66,13 @@ def tile_picked_maxsim_relu_p_kernel(tc, x_words, x_scales, d_words, d_scales, g
         for t in range(1, SLOTS):
             nc.sync.dma_start(w_raw[t][:], w_rows[t])
         load_words(x_word_tab, x_words)
-        nc.gpsimd.memset(gn_rows[:], 0.0)
+        nc.vector.memset(identity[:], 0.0)
         nc.scalar.dma_start(gn_rows[0:SLOTS, :], gn.rearrange("(b t r) o -> t b (r o)", t=SLOTS, r=8))
-        make_identity(nc, identity[:])
+        make_identity(nc, identity[:], nomemset=True)
         gn_bank = ps.tile([P, 2, HALF], F32, name="bank111")
         nc.tensor.transpose(gn_bank[:, 0, 0:P], gn_rows[:], identity[:])
         gn_sb = gn_bank[:, 0, 0:SLOTS]
 
-        planes = tile([P, 2 * H + S], U8, "planes")
-        nc.vector.memset(planes[:].bitcast(I32), 0)
 
         g_abs = tile([P, SLOTS], F32, "g_abs")
         g_step = tile([P, SLOTS], F32, "g_step")
@@ -81,7 +83,7 @@ def tile_picked_maxsim_relu_p_kernel(tc, x_words, x_scales, d_words, d_scales, g
 
         d_scale_got = tile([P, 2 * H], U8, "d_scale_got")
         x_scale_got = tile([P, S], U8, "x_scale_got")
-        scale_dealt = tile([P, 2 * H + S], U8, "x_scale_tab")
+        scale_dealt = tile_at(0, [P, 2 * H + S], U8, "scale_dealt")
         nc.vector.tensor_copy(d_scale_got[:, 0:H], d_scale_tab[:].indirect(k1_sb[:]))
         nc.vector.tensor_copy(d_scale_got[:, H : 2 * H], d_scale_tab[:].indirect(k2_sb[:]))
         nc.vector.tensor_copy(x_scale_got[:], x_scale_tab[:].indirect(offs_sb[:]))
@@ -90,10 +92,11 @@ def tile_picked_maxsim_relu_p_kernel(tc, x_words, x_scales, d_words, d_scales, g
             d_scale_got[:].bitcast(I32).rearrange("p (l b t w) -> p l t b w", l=2, t=SLOTS, w=2),
         )
         nc.vector.tensor_copy(scale_dealt[:, 2 * H :].bitcast(I32), x_scale_got[:].bitcast(I32))
-        for r in range(4):
-            nc.sync.dma_start(planes[:].bitcast(I32)[r:P:32, :], scale_dealt[:].bitcast(I32)[8 * r : P : 32, :])
+        planes = scale_dealt
+        for r in range(1, 4):
+            nc.sync.dma_start(planes[:].bitcast(I32)[r:P:32, :], planes[:].bitcast(I32)[8 * r : P : 32, :])
 
-        d_got = [tile([P, H], U32, name) for name in ("d_scale_got", "x_scale_got")]
+        d_got = [tile_at(2 * H + S, [P, H], U32, "d_word_got0"), tile([P, H], U32, "x_scale_got")]
         d_codes = [tile([P, H], U32, "d_codes%d" % side) for side in range(2)]
         for side, lst in enumerate((k1_sb, k2_sb)):
             nc.vector.tensor_copy(d_got[side][:], d_word_tab[:].indirect(lst[:]))
@@ -108,9 +111,9 @@ def tile_picked_maxsim_relu_p_kernel(tc, x_words, x_scales, d_words, d_scales, g
             nc.tensor.matmul_mx(
                 out=warm[:].rearrange("p u j -> p (u j)"),
                 lhsT=d_got[min(t, 1)][:, P * t : P * (t + 1)].bitcast(FP8X4),
-                lhsT_scale=scale_dealt[:, P * t : P * (t + 1)],
+                lhsT_scale=d_scale_got[:, P * t : P * (t + 1)],
                 rhs=d_got[0][:].bitcast(FP8X4),
-                rhs_scale=scale_dealt[:, 0:H],
+                rhs_scale=d_scale_got[:, 0:H],
                 start=True,
                 stop=True,
             )
@@ -194,7 +197,7 @@ def tile_picked_maxsim_relu_p_kernel(tc, x_words, x_scales, d_words, d_scales, g
                 nc.sync.dma_start(out_rows[v][:, :, j0 : j0 + width], res[:])
 
         names = [["bank%d%d%d" % (h, pair, side) for side in range(2) for pair in range(2)] for h in range(2)]
-        woven = [tile([P, HALF * SLOTS], BF16, "woven%d" % h) for h in range(2)]
+        woven = [tile([P, HALF * SLOTS], BF16, "woven0")]
         w_codes, w_plane = quantise("w", w_woven, N)
         relu_a(0)
         z0 = best("0", 0, 0, HALF)
@@ -212,6 +215,25 @@ def tile_picked_maxsim_relu_p_kernel(tc, x_words, x_scales, d_words, d_scales, g
         for t in range(1, SLOTS):
             best_slot(t)
         values("0", 0, HALF, *q0, names[0], (nc.scalar.copy,) * 4)
-        weave(nc.vector.tensor_copy, woven[1][:], z1[:])
-        q1 = quantise("1", woven[1], HALF)
-        values("1", HALF, HALF, *q1, names[1], (nc.scalar.copy, nc.vector.tensor_copy) * 2)
+        Q = HALF // 2
+        last = [tile([P, Q * SLOTS], BF16, "last%d" % c) for c in range(2)]
+        for c in range(2):
+            weave(nc.vector.tensor_copy, last[c][:], z1[:, :, Q * c : Q * (c + 1)])
+        q1 = [quantise("1%d" % c, last[c], Q) for c in range(2)]
+        out_rows = out.rearrange("(v p) j -> v p j", p=P)
+        last_banks = [ps.tile([P, 2, Q], F32, name=names[1][v]) for v in range(SLOTS)]
+        for c in range(2):
+            for v in range(SLOTS):
+                nc.tensor.matmul_mx(
+                    out=last_banks[v][:, c, :],
+                    lhsT=w_codes[:, P * v : P * (v + 1)].bitcast(FP8X4),
+                    lhsT_scale=w_plane[:, P * v : P * (v + 1)],
+                    rhs=q1[c][0][:].bitcast(FP8X4),
+                    rhs_scale=q1[c][1][:],
+                    start=True,
+                    stop=True,
+                )
+        for v in range(SLOTS):
+            res = tile([P, HALF], F32, "res1%d" % v)
+            (nc.scalar.copy, nc.vector.tensor_copy)[v % 2](res[:], last_banks[v][:].rearrange("p c j -> p (c j)"))
+            nc.sync.dma_start(out_rows[v][:, HALF:], res[:])

@@ -52,12 +52,13 @@ def tile_picked_maxsim_relu_p_kernel(tc, x_words, x_scales, d_words, d_scales, g
         def load_words(tab, words):
             nc.sync.dma_start(tab[:].bitcast(I32), words[0].rearrange("p n t -> p (n t)").bitcast(I32))
 
-        nc.vector.memset(d_scale_tab[:].bitcast(I32), 0)
         nc.vector.memset(gn_rows[:], 0.0)
+        nc.vector.memset(d_scale_tab[:].bitcast(I32), 0)
         nc.vector.memset(x_scale_tab[:].bitcast(I32), 0)
         w_rows = w1.rearrange("(b t r) m -> t b r m", t=SLOTS, r=8)
         nc.sync.dma_start(w_raw[0][:], w_rows[0])
         nc.sync.dma_start(k1_sb[:], k1)
+        nc.sync.dma_start(gn_rows[0:SLOTS, :], gn.rearrange("(b t r) o -> t b (r o)", t=SLOTS, r=8))
         load_scale_rows(nc.sync, d_scale_tab, d_scales)
         nc.sync.dma_start(k2_sb[:], k2)
         load_words(d_word_tab, d_words)
@@ -67,7 +68,6 @@ def tile_picked_maxsim_relu_p_kernel(tc, x_words, x_scales, d_words, d_scales, g
             nc.sync.dma_start(w_raw[t][:], w_rows[t])
         load_words(x_word_tab, x_words)
         nc.vector.memset(identity[:], 0.0)
-        nc.scalar.dma_start(gn_rows[0:SLOTS, :], gn.rearrange("(b t r) o -> t b (r o)", t=SLOTS, r=8))
         make_identity(nc, identity[:], nomemset=True)
         gn_bank = ps.tile([P, 2, HALF], F32, name="bank111")
         nc.tensor.transpose(gn_bank[:, 0, 0:P], gn_rows[:], identity[:])
@@ -123,8 +123,8 @@ def tile_picked_maxsim_relu_p_kernel(tc, x_words, x_scales, d_words, d_scales, g
         for t in range(SLOTS):
             nc.scalar.activation(w_signed[:, t, :], w_raw[t][:], ACT.Copy, scale=g_sign[:, t : t + 1])
         nc.scalar.copy(
-            w_woven[:].rearrange("p (c i t) -> p c t i", i=4, t=SLOTS),
-            w_signed[:].rearrange("p t (c i) -> p c t i", i=4),
+            w_woven[:].rearrange("p (m t) -> p m t", t=SLOTS),
+            w_signed[:].rearrange("p t m -> p m t"),
         )
 
         x_codes = []

@@ -153,11 +153,12 @@ def tile_picked_maxsim_relu_p_kernel(tc, x_words, x_scales, d_words, d_scales, g
             return banks
 
         banks = [scores(0), scores(1)]
-        ra = [[tile([P, HALF], F32, "ra%d%d" % (h, t)) for t in range(SLOTS)] for h in range(2)]
+        ra_tiles = [tile([P, SLOTS + 2 * h, HALF], (F32, BF16)[h], "ra%d" % h) for h in range(2)]
+        ra = [[ra_tiles[h][:, t, :] for t in range(SLOTS)] for h in range(2)]
 
         def relu_a(h):
             for t in range(SLOTS):
-                nc.scalar.activation(ra[h][t][:], banks[h][t // 2, 0][:, t % 2, :], ACT.Relu, scale=g_abs[:, t : t + 1])
+                nc.scalar.activation(ra[h][t], banks[h][t // 2, 0][:, t % 2, :], ACT.Relu, scale=g_abs[:, t : t + 1])
 
         def best(name, h, lo, width):
             z = tile([P, SLOTS, width], BF16, "z" + name)
@@ -168,7 +169,7 @@ def tile_picked_maxsim_relu_p_kernel(tc, x_words, x_scales, d_words, d_scales, g
             return z
 
         def weave(copy, woven, z):
-            copy(woven.rearrange("p (c i t) -> p c t i", i=4, t=SLOTS), z.rearrange("p t (c i) -> p c t i", i=4))
+            copy(woven.rearrange("p (j t) -> p j t", t=SLOTS), z.rearrange("p t j -> p j t"))
 
         def quantise(name, woven, width):
             codes = tile([P, width], U32, "codes" + name)
@@ -176,64 +177,52 @@ def tile_picked_maxsim_relu_p_kernel(tc, x_words, x_scales, d_words, d_scales, g
             nc.vector.quantize_mx(out=codes[:].bitcast(FP8X4), scales=plane[:], in_=woven[:])
             return codes, plane
 
-        def values(name, j0, width, codes, plane, bank_names, copy_engines):
-            group = SLOTS // len(bank_names)
-            out_rows = out.rearrange("(v u p) j -> v p u j", u=group, p=P)
-            for v, bank_name in enumerate(bank_names):
-                bank = ps.tile([P, group, width], F32, name=bank_name)
-                for u in range(group):
-                    m0 = P * (group * v + u)
+        names = [["bank%d%d%d" % (h, pair, side) for side in range(2) for pair in range(2)] for h in range(2)]
+        Q = HALF // 2
+        out_rows = out.rearrange("(v p) j -> v p j", p=P)
+
+        def weave_and_quantise(h, z):
+            woven = [tile([P, Q * SLOTS], BF16, "woven%d%d" % (h, c)) for c in range(2)]
+            for c in range(2):
+                weave(nc.vector.tensor_copy, woven[c][:], z[:, :, Q * c : Q * (c + 1)])
+            return [quantise("%d%d" % (h, c), woven[c], Q) for c in range(2)]
+
+        def values(h, quantised, copies, queues):
+            out_banks = [ps.tile([P, 2, Q], F32, name=names[h][v]) for v in range(SLOTS)]
+            for c in range(2):
+                for v in range(SLOTS):
                     nc.tensor.matmul_mx(
-                        out=bank[:, u, :],
-                        lhsT=w_codes[:, m0 : m0 + P].bitcast(FP8X4),
-                        lhsT_scale=w_plane[:, m0 : m0 + P],
-                        rhs=codes[:].bitcast(FP8X4),
-                        rhs_scale=plane[:],
+                        out=out_banks[v][:, c, :],
+                        lhsT=w_codes[:, P * v : P * (v + 1)].bitcast(FP8X4),
+                        lhsT_scale=w_plane[:, P * v : P * (v + 1)],
+                        rhs=quantised[c][0][:].bitcast(FP8X4),
+                        rhs_scale=quantised[c][1][:],
                         start=True,
                         stop=True,
                     )
-                res = tile([P, group, width], F32, "res%s%d" % (name, v))
-                copy_engines[v](res[:], bank[:])
-                nc.sync.dma_start(out_rows[v][:, :, j0 : j0 + width], res[:])
+            for v in range(SLOTS):
+                res = tile([P, HALF], F32, "res%d%d" % (h, v))
+                copies[v](res[:], out_banks[v][:].rearrange("p c j -> p (c j)"))
+                queues[v].dma_start(out_rows[v][:, HALF * h : HALF * (h + 1)], res[:])
 
-        names = [["bank%d%d%d" % (h, pair, side) for side in range(2) for pair in range(2)] for h in range(2)]
-        woven = [tile([P, HALF * SLOTS], BF16, "woven0")]
         w_codes, w_plane = quantise("w", w_woven, N)
         relu_a(0)
         z0 = best("0", 0, 0, HALF)
         relu_a(1)
-        weave(nc.vector.tensor_copy, woven[0][:], z0[:])
+        rb = ra_tiles[1][:, SLOTS:, :]
+        for t in range(2, SLOTS):
+            nc.scalar.activation(rb[:, t - 2, :], banks[1][1, 1][:, t - 2, :], ACT.Relu, scale=g_abs[:, t : t + 1])
         z1 = tile([P, SLOTS, HALF], BF16, "z1")
 
         def best_slot(t):
             nc.vector.scalar_tensor_tensor(
-                z1[:, t, :], banks[1][t // 2, 1][:, t % 2, :], g_abs[:, t : t + 1], ra[1][t][:], ALU.mult, ALU.max
+                z1[:, t, :], banks[1][t // 2, 1][:, t % 2, :], g_abs[:, t : t + 1], ra[1][t], ALU.mult, ALU.max
             )
 
         best_slot(0)
-        q0 = quantise("0", woven[0], HALF)
-        for t in range(1, SLOTS):
-            best_slot(t)
-        values("0", 0, HALF, *q0, names[0], (nc.scalar.copy,) * 4)
-        Q = HALF // 2
-        last = [tile([P, Q * SLOTS], BF16, "last%d" % c) for c in range(2)]
-        for c in range(2):
-            weave(nc.vector.tensor_copy, last[c][:], z1[:, :, Q * c : Q * (c + 1)])
-        q1 = [quantise("1%d" % c, last[c], Q) for c in range(2)]
-        out_rows = out.rearrange("(v p) j -> v p j", p=P)
-        last_banks = [ps.tile([P, 2, Q], F32, name=names[1][v]) for v in range(SLOTS)]
-        for c in range(2):
-            for v in range(SLOTS):
-                nc.tensor.matmul_mx(
-                    out=last_banks[v][:, c, :],
-                    lhsT=w_codes[:, P * v : P * (v + 1)].bitcast(FP8X4),
-                    lhsT_scale=w_plane[:, P * v : P * (v + 1)],
-                    rhs=q1[c][0][:].bitcast(FP8X4),
-                    rhs_scale=q1[c][1][:],
-                    start=True,
-                    stop=True,
-                )
-        for v in range(SLOTS):
-            res = tile([P, HALF], F32, "res1%d" % v)
-            (nc.scalar.copy, nc.vector.tensor_copy)[v % 2](res[:], last_banks[v][:].rearrange("p c j -> p (c j)"))
-            nc.sync.dma_start(out_rows[v][:, HALF:], res[:])
+        q0 = weave_and_quantise(0, z0)
+        values(0, q0, (nc.scalar.copy,) * 4, (nc.sync,) * 4)
+        best_slot(1)
+        nc.vector.tensor_tensor(z1[:, 2:, :], ra_tiles[1][:, 2:SLOTS, :], rb, ALU.max)
+        q1 = weave_and_quantise(1, z1)
+        values(1, q1, (nc.scalar.copy, nc.vector.tensor_copy) * 2, (nc.sync, nc.sync, nc.scalar, nc.sync))

@@ -110,7 +110,7 @@ def tile_picked_maxsim_relu_p_kernel(tc, x_words, x_scales, d_words, d_scales, g
         for t in range(3):
             nc.tensor.matmul_mx(
                 out=warm[:].rearrange("p u j -> p (u j)"),
-                lhsT=d_got[min(t, 1)][:, P * t : P * (t + 1)].bitcast(FP8X4),
+                lhsT=d_got[0][:, P * t : P * (t + 1)].bitcast(FP8X4),
                 lhsT_scale=d_scale_got[:, P * t : P * (t + 1)],
                 rhs=d_got[0][:].bitcast(FP8X4),
                 rhs_scale=d_scale_got[:, 0:H],
@@ -169,7 +169,7 @@ def tile_picked_maxsim_relu_p_kernel(tc, x_words, x_scales, d_words, d_scales, g
             return z
 
         def weave(copy, woven, z):
-            copy(woven.rearrange("p (j t) -> p j t", t=SLOTS), z.rearrange("p t j -> p j t"))
+            copy(woven.rearrange("p (c i t) -> p c t i", i=4, t=SLOTS), z.rearrange("p t (c i) -> p c t i", i=4))
 
         def quantise(name, woven, width):
             codes = tile([P, width], U32, "codes" + name)

@@ -16,7 +16,9 @@ ACT = mybir.ActivationFunctionType
 P = 128
 K, T, S, N, G, H = 512, 2048, 512, 512, 2048, 512
 SLOTS = 4
+RUN = 8
 HALF = S // 2
+QUARTER = S // 4
 SCORE_SCALE = 0.0625
 FLOPS = 2 * K * H * S * 2 + 2 * H * N * S
 
@@ -26,7 +28,6 @@ def tile_picked_maxsim_relu_p_kernel(tc, x_words, x_scales, d_words, d_scales, g
     with ExitStack() as ctx:
         sb = ctx.enter_context(tc.tile_pool(name="sb", bufs=1))
         ps = ctx.enter_context(tc.psum_pool(name="ps", bufs=1))
-
         reuse = ctx.enter_context(tc.tile_pool(name="reuse", bufs=1))
 
         def tile(shape, dtype, name):
@@ -46,8 +47,8 @@ def tile_picked_maxsim_relu_p_kernel(tc, x_words, x_scales, d_words, d_scales, g
         identity = tile([P, P], F32, "identity")
         w_raw = [tile([P, N], F32, "w_raw%d" % t) for t in range(SLOTS)]
 
-        def load_scale_rows(queue, tab, scales):
-            queue.dma_start(tab[:].bitcast(I32)[0:P:8, :], scales[0].bitcast(I32))
+        def load_scale_rows(tab, scales):
+            nc.sync.dma_start(tab[:].bitcast(I32)[0:P:RUN, :], scales[0].bitcast(I32))
 
         def load_words(tab, words):
             nc.sync.dma_start(tab[:].bitcast(I32), words[0].rearrange("p n t -> p (n t)").bitcast(I32))
@@ -55,76 +56,100 @@ def tile_picked_maxsim_relu_p_kernel(tc, x_words, x_scales, d_words, d_scales, g
         nc.vector.memset(gn_rows[:], 0.0)
         nc.vector.memset(d_scale_tab[:].bitcast(I32), 0)
         nc.vector.memset(x_scale_tab[:].bitcast(I32), 0)
-        w_rows = w1.rearrange("(b t r) m -> t b r m", t=SLOTS, r=8)
+        nc.vector.memset(identity[:], 0.0)
+        w_rows = w1.rearrange("(b t r) m -> t b r m", t=SLOTS, r=RUN)
         nc.sync.dma_start(w_raw[0][:], w_rows[0])
         nc.sync.dma_start(k1_sb[:], k1)
-        nc.sync.dma_start(gn_rows[0:SLOTS, :], gn.rearrange("(b t r) o -> t b (r o)", t=SLOTS, r=8))
-        load_scale_rows(nc.sync, d_scale_tab, d_scales)
+        nc.sync.dma_start(gn_rows[0:SLOTS, :], gn.rearrange("(b t r) o -> t b (r o)", t=SLOTS, r=RUN))
+        load_scale_rows(d_scale_tab, d_scales)
         nc.sync.dma_start(k2_sb[:], k2)
         load_words(d_word_tab, d_words)
         nc.sync.dma_start(offs_sb[:], offs)
-        load_scale_rows(nc.sync, x_scale_tab, x_scales)
+        load_scale_rows(x_scale_tab, x_scales)
         for t in range(1, SLOTS):
             nc.sync.dma_start(w_raw[t][:], w_rows[t])
         load_words(x_word_tab, x_words)
-        nc.vector.memset(identity[:], 0.0)
+
         make_identity(nc, identity[:], nomemset=True)
-        gn_bank = ps.tile([P, 2, HALF], F32, name="bank111")
+        gn_bank = ps.tile([P, 2, HALF], F32, name="bank_b11")
         nc.tensor.transpose(gn_bank[:, 0, 0:P], gn_rows[:], identity[:])
-        gn_sb = gn_bank[:, 0, 0:SLOTS]
-
-
+        gn_cols = gn_bank[:, 0, 0:SLOTS]
         g_abs = tile([P, SLOTS], F32, "g_abs")
         g_step = tile([P, SLOTS], F32, "g_step")
         g_sign = tile([P, SLOTS], F32, "g_sign")
-        nc.scalar.activation(g_step[:], gn_sb, ACT.Sign)
-        nc.scalar.activation(g_abs[:], gn_sb, ACT.Abs, scale=SCORE_SCALE)
+        nc.scalar.activation(g_step[:], gn_cols, ACT.Sign)
         nc.scalar.activation(g_sign[:], g_step[:], ACT.Sign, bias=0.5)
+        nc.scalar.activation(g_abs[:], gn_cols, ACT.Abs, scale=SCORE_SCALE)
 
         d_scale_got = tile([P, 2 * H], U8, "d_scale_got")
         x_scale_got = tile([P, S], U8, "x_scale_got")
-        scale_dealt = tile_at(0, [P, 2 * H + S], U8, "scale_dealt")
+        planes = tile_at(0, [P, 2 * H + S], U8, "planes")
         nc.vector.tensor_copy(d_scale_got[:, 0:H], d_scale_tab[:].indirect(k1_sb[:]))
         nc.vector.tensor_copy(d_scale_got[:, H : 2 * H], d_scale_tab[:].indirect(k2_sb[:]))
         nc.vector.tensor_copy(x_scale_got[:], x_scale_tab[:].indirect(offs_sb[:]))
         nc.vector.tensor_copy(
-            scale_dealt[:, 0 : 2 * H].bitcast(I32).rearrange("p (l t b w) -> p l t b w", l=2, t=SLOTS, w=2),
+            planes[:, 0 : 2 * H].bitcast(I32).rearrange("p (l t b w) -> p l t b w", l=2, t=SLOTS, w=2),
             d_scale_got[:].bitcast(I32).rearrange("p (l b t w) -> p l t b w", l=2, t=SLOTS, w=2),
         )
-        nc.vector.tensor_copy(scale_dealt[:, 2 * H :].bitcast(I32), x_scale_got[:].bitcast(I32))
-        planes = scale_dealt
+        nc.vector.tensor_copy(planes[:, 2 * H :].bitcast(I32), x_scale_got[:].bitcast(I32))
         for r in range(1, 4):
-            nc.sync.dma_start(planes[:].bitcast(I32)[r:P:32, :], planes[:].bitcast(I32)[8 * r : P : 32, :])
-
-        d_got = [tile_at(2 * H + S, [P, H], U32, "d_word_got0"), tile([P, H], U32, "x_scale_got")]
-        d_codes = [tile([P, H], U32, "d_codes%d" % side) for side in range(2)]
-        for side, lst in enumerate((k1_sb, k2_sb)):
-            nc.vector.tensor_copy(d_got[side][:], d_word_tab[:].indirect(lst[:]))
-        for side in range(2):
-            nc.vector.tensor_copy(
-                d_codes[side][:].bitcast(I32).rearrange("p (t b r) -> p t b r", t=SLOTS, r=8),
-                d_got[side][:].bitcast(I32).rearrange("p (b t r) -> p t b r", t=SLOTS, r=8),
-            )
-
-        warm = ps.tile([P, 2, HALF], F32, name="bank111")
-        for t in range(3):
-            nc.tensor.matmul_mx(
-                out=warm[:].rearrange("p u j -> p (u j)"),
-                lhsT=d_got[0][:, P * t : P * (t + 1)].bitcast(FP8X4),
-                lhsT_scale=d_scale_got[:, P * t : P * (t + 1)],
-                rhs=d_got[0][:].bitcast(FP8X4),
-                rhs_scale=d_scale_got[:, 0:H],
-                start=True,
-                stop=True,
-            )
+            nc.sync.dma_start(planes[:].bitcast(I32)[r:P:32, :], planes[:].bitcast(I32)[RUN * r : P : 32, :])
 
         w_signed = tile([P, SLOTS, N], BF16, "w_signed")
-        w_woven = tile([P, N * SLOTS], BF16, "w_woven")
+        w_woven = tile([P, SLOTS * N], BF16, "w_woven")
         for t in range(SLOTS):
             nc.scalar.activation(w_signed[:, t, :], w_raw[t][:], ACT.Copy, scale=g_sign[:, t : t + 1])
-        nc.scalar.copy(
-            w_woven[:].rearrange("p (m t) -> p m t", t=SLOTS),
-            w_signed[:].rearrange("p t m -> p m t"),
+        nc.scalar.copy(w_woven[:].rearrange("p (m t) -> p m t", t=SLOTS), w_signed[:].rearrange("p t m -> p m t"))
+
+        def deal(codes, got):
+            nc.vector.tensor_copy(
+                codes[:].bitcast(I32).rearrange("p (t b r) -> p t b r", t=SLOTS, r=RUN),
+                got[:].bitcast(I32).rearrange("p (b t r) -> p t b r", t=SLOTS, r=RUN),
+            )
+            return codes
+
+        def quantise(codes, woven, name):
+            plane = tile([P, woven.shape[1] // SLOTS], U8, name)
+            nc.vector.quantize_mx(out=codes[:].bitcast(FP8X4), scales=plane[:], in_=woven[:])
+            return codes, plane
+
+        def scores(h):
+            banks = {}
+            for pair in range(2):
+                for side in range(2):
+                    bank = ps.tile([P, 2, HALF], F32, name="bank_%s%d%d" % ("ab"[side], h, pair))
+                    for u in range(2):
+                        t = 2 * pair + u
+                        nc.tensor.matmul_mx(
+                            out=bank[:, u, :],
+                            lhsT=key_codes[side][:, P * t : P * (t + 1)].bitcast(FP8X4),
+                            lhsT_scale=planes[:, side * H + P * t : side * H + P * (t + 1)],
+                            rhs=x_codes[h][:].bitcast(FP8X4),
+                            rhs_scale=planes[:, 2 * H + HALF * h : 2 * H + HALF * (h + 1)],
+                            start=True,
+                            stop=True,
+                        )
+                    banks[side, pair] = bank
+            return [[banks[side, t // 2][:, t % 2, :] for t in range(SLOTS)] for side in range(2)]
+
+        def relu_out(dst, score, slots):
+            for i, t in enumerate(slots):
+                nc.scalar.activation(dst[:, i, :], score[t], ACT.Relu, scale=g_abs[:, t : t + 1])
+
+        key_got = [tile_at(2 * H + S, [P, H], U32, "a_got"), tile([P, H], U32, "x_scale_got")]
+        for got, key_list in zip(key_got, (k1_sb, k2_sb)):
+            nc.vector.tensor_copy(got[:], d_word_tab[:].indirect(key_list[:]))
+        key_codes = [deal(tile([P, H], U32, name), got) for name, got in zip(("a_codes", "b_codes"), key_got)]
+
+        warm_bank = ps.tile([P, 2, HALF], F32, name="bank_b11")
+        nc.tensor.matmul_mx(
+            out=warm_bank[:].rearrange("p u j -> p (u j)"),
+            lhsT=key_codes[0][:, 0:P].bitcast(FP8X4),
+            lhsT_scale=d_scale_got[:, 0:P],
+            rhs=key_codes[0][:].bitcast(FP8X4),
+            rhs_scale=d_scale_got[:, 0:H],
+            start=True,
+            stop=True,
         )
 
         x_codes = []
@@ -132,97 +157,57 @@ def tile_picked_maxsim_relu_p_kernel(tc, x_words, x_scales, d_words, d_scales, g
             got = tile([P, HALF], U32, "x_codes%d" % h)
             nc.vector.tensor_copy(got[:], x_word_tab[:].indirect(offs_sb[:, 16 * h : 16 * (h + 1)]))
             x_codes.append(got)
+        w_codes, w_plane = quantise(tile([P, N], U32, "w_codes"), w_woven, "w_plane")
 
-        def scores(h):
-            banks = {}
-            for pair in range(2):
-                for side in range(2):
-                    bank = ps.tile([P, 2, HALF], F32, name="bank%d%d%d" % (h, pair, side))
-                    for u in range(2):
-                        t = 2 * pair + u
-                        nc.tensor.matmul_mx(
-                            out=bank[:, u, :],
-                            lhsT=d_codes[side][:, P * t : P * (t + 1)].bitcast(FP8X4),
-                            lhsT_scale=planes[:, side * H + P * t : side * H + P * (t + 1)],
-                            rhs=x_codes[h][:].bitcast(FP8X4),
-                            rhs_scale=planes[:, 2 * H + HALF * h : 2 * H + HALF * (h + 1)],
-                            start=True,
-                            stop=True,
-                        )
-                    banks[pair, side] = bank
-            return banks
+        ra = [tile([P, SLOTS, HALF], BF16, "ra%d" % h) for h in range(2)]
+        z = [tile([P, SLOTS, HALF], BF16, "z%d" % h) for h in range(2)]
+        rb = tile([P, 2, HALF], BF16, "rb")
 
-        banks = [scores(0), scores(1)]
-        ra_tiles = [tile([P, SLOTS + 2 * h, HALF], (F32, BF16)[h], "ra%d" % h) for h in range(2)]
-        ra = [[ra_tiles[h][:, t, :] for t in range(SLOTS)] for h in range(2)]
+        def best(h, t, b_scores):
+            nc.vector.scalar_tensor_tensor(z[h][:, t, :], b_scores[t], g_abs[:, t : t + 1], ra[h][:, t, :], ALU.mult, ALU.max)
 
-        def relu_a(h):
-            for t in range(SLOTS):
-                nc.scalar.activation(ra[h][t], banks[h][t // 2, 0][:, t % 2, :], ACT.Relu, scale=g_abs[:, t : t + 1])
+        a_scores, b_scores = scores(0)
+        relu_out(ra[0], a_scores, range(SLOTS))
+        for t in range(SLOTS):
+            best(0, t, b_scores)
+        a_scores, b_scores = scores(1)
+        relu_out(ra[1], a_scores, range(SLOTS))
+        relu_out(rb, b_scores, range(2, SLOTS))
+        best(1, 0, b_scores)
 
-        def best(name, h, lo, width):
-            z = tile([P, SLOTS, width], BF16, "z" + name)
-            for t in range(SLOTS):
-                nc.vector.scalar_tensor_tensor(
-                    z[:, t, :], banks[h][t // 2, 1][:, t % 2, lo : lo + width], g_abs[:, t : t + 1], ra[h][t][:, lo : lo + width], ALU.mult, ALU.max
-                )
-            return z
-
-        def weave(copy, woven, z):
-            copy(woven.rearrange("p (c i t) -> p c t i", i=4, t=SLOTS), z.rearrange("p t (c i) -> p c t i", i=4))
-
-        def quantise(name, woven, width):
-            codes = tile([P, width], U32, "codes" + name)
-            plane = tile([P, width], U8, "plane" + name)
-            nc.vector.quantize_mx(out=codes[:].bitcast(FP8X4), scales=plane[:], in_=woven[:])
-            return codes, plane
-
-        names = [["bank%d%d%d" % (h, pair, side) for side in range(2) for pair in range(2)] for h in range(2)]
-        Q = HALF // 2
         out_rows = out.rearrange("(v p) j -> v p j", p=P)
 
-        def weave_and_quantise(h, z):
-            woven = [tile([P, Q * SLOTS], BF16, "woven%d%d" % (h, c)) for c in range(2)]
+        def weave_and_quantise(h):
+            woven = [tile([P, QUARTER * SLOTS], BF16, "z_woven%d%d" % (h, c)) for c in range(2)]
             for c in range(2):
-                weave(nc.vector.tensor_copy, woven[c][:], z[:, :, Q * c : Q * (c + 1)])
-            return [quantise("%d%d" % (h, c), woven[c], Q) for c in range(2)]
+                nc.vector.tensor_copy(
+                    woven[c][:].rearrange("p (c i t) -> p c t i", i=4, t=SLOTS),
+                    z[h][:, :, QUARTER * c : QUARTER * (c + 1)].rearrange("p t (c i) -> p c t i", i=4),
+                )
+            return [quantise(tile([P, QUARTER], U32, "z_codes%d%d" % (h, c)), woven[c], "z_plane%d%d" % (h, c)) for c in range(2)]
 
-        def values(h, quantised, copies, queues):
-            out_banks = [ps.tile([P, 2, Q], F32, name=names[h][v]) for v in range(SLOTS)]
+        def values(h, z_mx, copies, queues):
+            banks = [ps.tile([P, 2, QUARTER], F32, name="bank_%s%d%d" % ("ab"[v // 2], h, v % 2)) for v in range(SLOTS)]
             for c in range(2):
                 for v in range(SLOTS):
+                    cols = slice(P * v, P * (v + 1))
                     nc.tensor.matmul_mx(
-                        out=out_banks[v][:, c, :],
-                        lhsT=w_codes[:, P * v : P * (v + 1)].bitcast(FP8X4),
-                        lhsT_scale=w_plane[:, P * v : P * (v + 1)],
-                        rhs=quantised[c][0][:].bitcast(FP8X4),
-                        rhs_scale=quantised[c][1][:],
+                        out=banks[v][:, c, :],
+                        lhsT=w_codes[:, cols].bitcast(FP8X4),
+                        lhsT_scale=w_plane[:, cols],
+                        rhs=z_mx[c][0][:].bitcast(FP8X4),
+                        rhs_scale=z_mx[c][1][:],
                         start=True,
                         stop=True,
                     )
             for v in range(SLOTS):
                 res = tile([P, HALF], F32, "res%d%d" % (h, v))
-                copies[v](res[:], out_banks[v][:].rearrange("p c j -> p (c j)"))
+                copies[v](res[:], banks[v][:].rearrange("p c j -> p (c j)"))
                 queues[v].dma_start(out_rows[v][:, HALF * h : HALF * (h + 1)], res[:])
 
-        w_codes, w_plane = quantise("w", w_woven, N)
-        relu_a(0)
-        z0 = best("0", 0, 0, HALF)
-        relu_a(1)
-        rb = ra_tiles[1][:, SLOTS:, :]
-        for t in range(2, SLOTS):
-            nc.scalar.activation(rb[:, t - 2, :], banks[1][1, 1][:, t - 2, :], ACT.Relu, scale=g_abs[:, t : t + 1])
-        z1 = tile([P, SLOTS, HALF], BF16, "z1")
-
-        def best_slot(t):
-            nc.vector.scalar_tensor_tensor(
-                z1[:, t, :], banks[1][t // 2, 1][:, t % 2, :], g_abs[:, t : t + 1], ra[1][t], ALU.mult, ALU.max
-            )
-
-        best_slot(0)
-        q0 = weave_and_quantise(0, z0)
-        values(0, q0, (nc.scalar.copy,) * 4, (nc.sync,) * 4)
-        best_slot(1)
-        nc.vector.tensor_tensor(z1[:, 2:, :], ra_tiles[1][:, 2:SLOTS, :], rb, ALU.max)
-        q1 = weave_and_quantise(1, z1)
-        values(1, q1, (nc.scalar.copy, nc.vector.tensor_copy) * 2, (nc.sync, nc.sync, nc.scalar, nc.sync))
+        values(0, weave_and_quantise(0), (nc.scalar.copy,) * 4, (nc.sync,) * 4)
+        best(1, 1, b_scores)
+        for c in range(2):
+            cols = slice(QUARTER * c, QUARTER * (c + 1))
+            nc.vector.tensor_tensor(z[1][:, 2:, cols], ra[1][:, 2:, cols], rb[:, :, cols], ALU.max)
+        values(1, weave_and_quantise(1), (nc.scalar.copy, nc.vector.tensor_copy) * 2, (nc.sync, nc.sync, nc.scalar, nc.sync))

@@ -19,6 +19,8 @@ SLOTS = 4
 RUN = 8
 HALF = S // 2
 QUARTER = S // 4
+WARM_ROWS = 32
+WARM_PASSES = 4
 SCORE_SCALE = 0.0625
 FLOPS = 2 * K * H * S * 2 + 2 * H * N * S
 
@@ -43,7 +45,7 @@ def tile_picked_maxsim_relu_p_kernel(tc, x_words, x_scales, d_words, d_scales, g
         x_scale_tab = tile_at(0, [P, T], U8, "x_scale_tab")
         d_word_tab = tile([P, G], U32, "d_word_tab")
         x_word_tab = tile([P, T], U32, "x_word_tab")
-        gn_rows = tile([P, P], F32, "gn_rows")
+        gn_blocks = tile([P, SLOTS, RUN], F32, "gn_blocks")
         identity = tile([P, P], F32, "identity")
         w_raw = [tile([P, N], F32, "w_raw%d" % t) for t in range(SLOTS)]
 
@@ -53,14 +55,16 @@ def tile_picked_maxsim_relu_p_kernel(tc, x_words, x_scales, d_words, d_scales, g
         def load_words(tab, words):
             nc.sync.dma_start(tab[:].bitcast(I32), words[0].rearrange("p n t -> p (n t)").bitcast(I32))
 
-        nc.vector.memset(gn_rows[:], 0.0)
+        nc.vector.memset(identity[:], 0.0)
         nc.vector.memset(d_scale_tab[:].bitcast(I32), 0)
         nc.vector.memset(x_scale_tab[:].bitcast(I32), 0)
-        nc.vector.memset(identity[:], 0.0)
         w_rows = w1.rearrange("(b t r) m -> t b r m", t=SLOTS, r=RUN)
         nc.sync.dma_start(w_raw[0][:], w_rows[0])
         nc.sync.dma_start(k1_sb[:], k1)
-        nc.sync.dma_start(gn_rows[0:SLOTS, :], gn.rearrange("(b t r) o -> t b (r o)", t=SLOTS, r=RUN))
+        nc.sync.dma_start(
+            gn_blocks[:].rearrange("p t r -> p (t r)"),
+            gn.rearrange("(b c) o -> b o c", c=SLOTS * RUN).to_broadcast([P // RUN, RUN, SLOTS * RUN]),
+        )
         load_scale_rows(d_scale_tab, d_scales)
         nc.sync.dma_start(k2_sb[:], k2)
         load_words(d_word_tab, d_words)
@@ -71,9 +75,19 @@ def tile_picked_maxsim_relu_p_kernel(tc, x_words, x_scales, d_words, d_scales, g
         load_words(x_word_tab, x_words)
 
         make_identity(nc, identity[:], nomemset=True)
-        gn_bank = ps.tile([P, 2, HALF], F32, name="bank_b11")
-        nc.tensor.transpose(gn_bank[:, 0, 0:P], gn_rows[:], identity[:])
-        gn_cols = gn_bank[:, 0, 0:SLOTS]
+
+        def fold(name, values, width):
+            while values.shape[2] > width:
+                half = values.shape[2] // 2
+                summed = tile([P, values.shape[1], half], F32, "%s%d" % (name, half))
+                nc.gpsimd.tensor_tensor(summed[:], values[:, :, 0:half], values[:, :, half:], ALU.add)
+                values = summed[:]
+            return values
+
+        own_place = fold("own_place", identity[:].unsqueeze(1), RUN)
+        gn_masked = tile([P, SLOTS, RUN], F32, "gn_masked")
+        nc.gpsimd.tensor_tensor(gn_masked[:], gn_blocks[:], own_place.to_broadcast([P, SLOTS, RUN]), ALU.mult)
+        gn_cols = fold("gn_sum", gn_masked[:], 1).rearrange("p t o -> p (t o)")
         g_abs = tile([P, SLOTS], F32, "g_abs")
         g_step = tile([P, SLOTS], F32, "g_step")
         g_sign = tile([P, SLOTS], F32, "g_sign")
@@ -141,16 +155,17 @@ def tile_picked_maxsim_relu_p_kernel(tc, x_words, x_scales, d_words, d_scales, g
             nc.vector.tensor_copy(got[:], d_word_tab[:].indirect(key_list[:]))
         key_codes = [deal(tile([P, H], U32, name), got) for name, got in zip(("a_codes", "b_codes"), key_got)]
 
-        warm_bank = ps.tile([P, 2, HALF], F32, name="bank_b11")
-        nc.tensor.matmul_mx(
-            out=warm_bank[:].rearrange("p u j -> p (u j)"),
-            lhsT=key_codes[0][:, 0:P].bitcast(FP8X4),
-            lhsT_scale=d_scale_got[:, 0:P],
-            rhs=key_codes[0][:].bitcast(FP8X4),
-            rhs_scale=d_scale_got[:, 0:H],
-            start=True,
-            stop=True,
-        )
+        warm_bank = ps.tile([WARM_ROWS, H], F32, name="bank_b11")
+        for i in range(WARM_PASSES):
+            nc.tensor.matmul_mx(
+                out=warm_bank[:],
+                lhsT=key_got[0][:, 0:WARM_ROWS].bitcast(FP8X4),
+                lhsT_scale=d_scale_got[:, 0:WARM_ROWS],
+                rhs=key_got[0][:].bitcast(FP8X4),
+                rhs_scale=d_scale_got[:, 0:H],
+                start=True,
+                stop=True,
+            )
 
         x_codes = []
         for h in range(2):

@@ -55,8 +55,8 @@ def tile_picked_maxsim_relu_p_kernel(tc, x_words, x_scales, d_words, d_scales, g
         def load_words(tab, words):
             nc.sync.dma_start(tab[:].bitcast(I32), words[0].rearrange("p n t -> p (n t)").bitcast(I32))
 
-        nc.vector.memset(identity[:], 0.0)
         nc.vector.memset(d_scale_tab[:].bitcast(I32), 0)
+        nc.vector.memset(identity[:], 0.0)
         nc.vector.memset(x_scale_tab[:].bitcast(I32), 0)
         w_rows = w1.rearrange("(b t r) m -> t b r m", t=SLOTS, r=RUN)
         nc.sync.dma_start(w_raw[0][:], w_rows[0])
@@ -65,8 +65,8 @@ def tile_picked_maxsim_relu_p_kernel(tc, x_words, x_scales, d_words, d_scales, g
             gn_blocks[:].rearrange("p t r -> p (t r)"),
             gn.rearrange("(b c) o -> b o c", c=SLOTS * RUN).to_broadcast([P // RUN, RUN, SLOTS * RUN]),
         )
-        load_scale_rows(d_scale_tab, d_scales)
         nc.sync.dma_start(k2_sb[:], k2)
+        load_scale_rows(d_scale_tab, d_scales)
         load_words(d_word_tab, d_words)
         nc.sync.dma_start(offs_sb[:], offs)
         load_scale_rows(x_scale_tab, x_scales)
@@ -76,24 +76,21 @@ def tile_picked_maxsim_relu_p_kernel(tc, x_words, x_scales, d_words, d_scales, g
 
         make_identity(nc, identity[:], nomemset=True)
 
-        def fold(name, values, width):
-            while values.shape[2] > width:
-                half = values.shape[2] // 2
-                summed = tile([P, values.shape[1], half], F32, "%s%d" % (name, half))
-                nc.gpsimd.tensor_tensor(summed[:], values[:, :, 0:half], values[:, :, half:], ALU.add)
-                values = summed[:]
-            return values
-
-        own_place = fold("own_place", identity[:].unsqueeze(1), RUN)
+        own_place = identity[:]
+        while own_place.shape[1] > RUN:
+            width = own_place.shape[1] // 2
+            summed = tile([P, width], F32, "own_place%d" % width)
+            nc.gpsimd.tensor_tensor(summed[:], own_place[:, 0:width], own_place[:, width:], ALU.add)
+            own_place = summed[:]
         gn_masked = tile([P, SLOTS, RUN], F32, "gn_masked")
-        nc.gpsimd.tensor_tensor(gn_masked[:], gn_blocks[:], own_place.to_broadcast([P, SLOTS, RUN]), ALU.mult)
-        gn_cols = fold("gn_sum", gn_masked[:], 1).rearrange("p t o -> p (t o)")
+        nc.gpsimd.tensor_tensor(gn_masked[:], gn_blocks[:], own_place.unsqueeze(1).to_broadcast([P, SLOTS, RUN]), ALU.mult)
         g_abs = tile([P, SLOTS], F32, "g_abs")
         g_step = tile([P, SLOTS], F32, "g_step")
         g_sign = tile([P, SLOTS], F32, "g_sign")
-        nc.scalar.activation(g_step[:], gn_cols, ACT.Sign)
+        summands = tile([P, 2, SLOTS, RUN], F32, "summands")
+        for t in range(SLOTS):
+            nc.scalar.activation(summands[:, 0, t, :], gn_masked[:, t, :], ACT.Sign, accum_out=g_step[:, t : t + 1])
         nc.scalar.activation(g_sign[:], g_step[:], ACT.Sign, bias=0.5)
-        nc.scalar.activation(g_abs[:], gn_cols, ACT.Abs, scale=SCORE_SCALE)
 
         d_scale_got = tile([P, 2 * H], U8, "d_scale_got")
         x_scale_got = tile([P, S], U8, "x_scale_got")
@@ -114,6 +111,8 @@ def tile_picked_maxsim_relu_p_kernel(tc, x_words, x_scales, d_words, d_scales, g
         for t in range(SLOTS):
             nc.scalar.activation(w_signed[:, t, :], w_raw[t][:], ACT.Copy, scale=g_sign[:, t : t + 1])
         nc.scalar.copy(w_woven[:].rearrange("p (m t) -> p m t", t=SLOTS), w_signed[:].rearrange("p t m -> p m t"))
+        for t in range(SLOTS):
+            nc.scalar.activation(summands[:, 1, t, :], gn_masked[:, t, :], ACT.Abs, scale=SCORE_SCALE, accum_out=g_abs[:, t : t + 1])
 
         def deal(codes, got):
             nc.vector.tensor_copy(

@@ -20,7 +20,6 @@ RUN = 8
 HALF = S // 2
 QUARTER = S // 4
 WARM_ROWS = 32
-WARM_PASSES = 4
 SCORE_SCALE = 0.0625
 FLOPS = 2 * K * H * S * 2 + 2 * H * N * S
 
@@ -154,17 +153,20 @@ def tile_picked_maxsim_relu_p_kernel(tc, x_words, x_scales, d_words, d_scales, g
             nc.vector.tensor_copy(got[:], d_word_tab[:].indirect(key_list[:]))
         key_codes = [deal(tile([P, H], U32, name), got) for name, got in zip(("a_codes", "b_codes"), key_got)]
 
-        warm_bank = ps.tile([WARM_ROWS, H], F32, name="bank_b11")
-        for i in range(WARM_PASSES):
-            nc.tensor.matmul_mx(
-                out=warm_bank[:],
-                lhsT=key_got[0][:, 0:WARM_ROWS].bitcast(FP8X4),
-                lhsT_scale=d_scale_got[:, 0:WARM_ROWS],
-                rhs=key_got[0][:].bitcast(FP8X4),
-                rhs_scale=d_scale_got[:, 0:H],
-                start=True,
-                stop=True,
-            )
+        def warm_up(bank_name, passes):
+            warm_bank = ps.tile([WARM_ROWS, H], F32, name=bank_name)
+            for i in range(passes):
+                nc.tensor.matmul_mx(
+                    out=warm_bank[:],
+                    lhsT=key_got[0][:, 0:WARM_ROWS].bitcast(FP8X4),
+                    lhsT_scale=d_scale_got[:, 0:WARM_ROWS],
+                    rhs=key_got[0][:].bitcast(FP8X4),
+                    rhs_scale=d_scale_got[:, 0:H],
+                    start=True,
+                    stop=True,
+                )
+
+        warm_up("bank_b11", 3)
 
         x_codes = []
         for h in range(2):
@@ -187,6 +189,7 @@ def tile_picked_maxsim_relu_p_kernel(tc, x_words, x_scales, d_words, d_scales, g
         a_scores, b_scores = scores(1)
         relu_out(ra[1], a_scores, range(SLOTS))
         relu_out(rb, b_scores, range(2, SLOTS))
+        warm_up("bank_a11", 1)
         best(1, 0, b_scores)
 
         out_rows = out.rearrange("(v p) j -> v p j", p=P)

@@ -66,11 +66,11 @@ def tile_picked_maxsim_relu_p_kernel(tc, x_words, x_scales, d_words, d_scales, g
         )
         nc.sync.dma_start(k2_sb[:], k2)
         load_scale_rows(d_scale_tab, d_scales)
-        load_words(d_word_tab, d_words)
-        nc.sync.dma_start(offs_sb[:], offs)
-        load_scale_rows(x_scale_tab, x_scales)
         for t in range(1, SLOTS):
             nc.sync.dma_start(w_raw[t][:], w_rows[t])
+        nc.sync.dma_start(offs_sb[:], offs)
+        load_scale_rows(x_scale_tab, x_scales)
+        load_words(d_word_tab, d_words)
         load_words(x_word_tab, x_words)
 
         make_identity(nc, identity[:], nomemset=True)

@@ -20,6 +20,10 @@ RUN = 8
 HALF = S // 2
 QUARTER = S // 4
 WARM_ROWS = 32
+W_RAW_AT = (0, 3328, 12288, 7936)
+EARLY = 384
+LATE = N - EARLY
+SCALE_GOT_AT = 14336
 SCORE_SCALE = 0.0625
 FLOPS = 2 * K * H * S * 2 + 2 * H * N * S
 
@@ -41,12 +45,12 @@ def tile_picked_maxsim_relu_p_kernel(tc, x_words, x_scales, d_words, d_scales, g
         k2_sb = tile([P, H // 16], U16, "k2_sb")
         offs_sb = tile([P, S // 16], U16, "offs_sb")
         d_scale_tab = tile([P, G], U8, "d_scale_tab")
-        x_scale_tab = tile_at(0, [P, T], U8, "x_scale_tab")
+        x_scale_tab = tile([P, T], U8, "x_scale_tab")
         d_word_tab = tile([P, G], U32, "d_word_tab")
         x_word_tab = tile([P, T], U32, "x_word_tab")
         gn_blocks = tile([P, SLOTS, RUN], F32, "gn_blocks")
         identity = tile([P, P], F32, "identity")
-        w_raw = [tile([P, N], F32, "w_raw%d" % t) for t in range(SLOTS)]
+        w_raw = [tile_at(W_RAW_AT[t], [P, EARLY], F32, "w_raw%d" % t) for t in range(SLOTS)]
 
         def load_scale_rows(tab, scales):
             nc.sync.dma_start(tab[:].bitcast(I32)[0:P:RUN, :], scales[0].bitcast(I32))
@@ -58,7 +62,7 @@ def tile_picked_maxsim_relu_p_kernel(tc, x_words, x_scales, d_words, d_scales, g
         nc.vector.memset(identity[:], 0.0)
         nc.vector.memset(x_scale_tab[:].bitcast(I32), 0)
         w_rows = w1.rearrange("(b t r) m -> t b r m", t=SLOTS, r=RUN)
-        nc.sync.dma_start(w_raw[0][:], w_rows[0])
+        nc.sync.dma_start(w_raw[0][:], w_rows[0][:, :, 0:EARLY])
         nc.sync.dma_start(k1_sb[:], k1)
         nc.sync.dma_start(
             gn_blocks[:].rearrange("p t r -> p (t r)"),
@@ -67,7 +71,7 @@ def tile_picked_maxsim_relu_p_kernel(tc, x_words, x_scales, d_words, d_scales, g
         nc.sync.dma_start(k2_sb[:], k2)
         load_scale_rows(d_scale_tab, d_scales)
         for t in range(1, SLOTS):
-            nc.sync.dma_start(w_raw[t][:], w_rows[t])
+            nc.sync.dma_start(w_raw[t][:], w_rows[t][:, :, 0:EARLY])
         nc.sync.dma_start(offs_sb[:], offs)
         load_scale_rows(x_scale_tab, x_scales)
         load_words(d_word_tab, d_words)
@@ -92,7 +96,7 @@ def tile_picked_maxsim_relu_p_kernel(tc, x_words, x_scales, d_words, d_scales, g
         nc.scalar.activation(g_sign[:], g_step[:], ACT.Sign, bias=0.5)
 
         d_scale_got = tile([P, 2 * H], U8, "d_scale_got")
-        x_scale_got = tile([P, S], U8, "x_scale_got")
+        x_scale_got = tile_at(SCALE_GOT_AT, [P, S], U8, "x_scale_got")
         planes = tile_at(0, [P, 2 * H + S], U8, "planes")
         nc.vector.tensor_copy(d_scale_got[:, 0:H], d_scale_tab[:].indirect(k1_sb[:]))
         nc.vector.tensor_copy(d_scale_got[:, H : 2 * H], d_scale_tab[:].indirect(k2_sb[:]))
@@ -104,14 +108,27 @@ def tile_picked_maxsim_relu_p_kernel(tc, x_words, x_scales, d_words, d_scales, g
         nc.vector.tensor_copy(planes[:, 2 * H :].bitcast(I32), x_scale_got[:].bitcast(I32))
         for r in range(1, 4):
             nc.sync.dma_start(planes[:].bitcast(I32)[r:P:32, :], planes[:].bitcast(I32)[RUN * r : P : 32, :])
+        w_late = tile_at(SCALE_GOT_AT, [P, SLOTS, LATE], F32, "w_late")
+        for t in range(SLOTS):
+            nc.sync.dma_start(w_late[:, t, :], w_rows[t][:, :, EARLY:])
 
-        w_signed = tile([P, SLOTS, N], BF16, "w_signed")
-        w_woven = tile([P, SLOTS * N], BF16, "w_woven")
+        w_signed = tile([P, SLOTS, EARLY], BF16, "w_signed")
+        w_woven = tile([P, SLOTS * EARLY], BF16, "w_woven")
         for t in range(SLOTS):
             nc.scalar.activation(w_signed[:, t, :], w_raw[t][:], ACT.Copy, scale=g_sign[:, t : t + 1])
         nc.scalar.copy(w_woven[:].rearrange("p (m t) -> p m t", t=SLOTS), w_signed[:].rearrange("p t m -> p m t"))
         for t in range(SLOTS):
             nc.scalar.activation(summands[:, 1, t, :], gn_masked[:, t, :], ACT.Abs, scale=SCORE_SCALE, accum_out=g_abs[:, t : t + 1])
+
+        w_late_woven = tile([P, SLOTS * LATE], BF16, "w_late_woven")
+        piece = LATE // 2
+        for c in range(2):
+            nc.gpsimd.tensor_tensor(
+                w_late_woven[:].rearrange("p (m t) -> p m t", t=SLOTS)[:, piece * c : piece * (c + 1), :],
+                w_late[:, :, piece * c : piece * (c + 1)].rearrange("p t m -> p m t"),
+                g_sign[:].unsqueeze(1).to_broadcast([P, piece, SLOTS]),
+                ALU.mult,
+            )
 
         def deal(codes, got):
             nc.vector.tensor_copy(
@@ -148,10 +165,10 @@ def tile_picked_maxsim_relu_p_kernel(tc, x_words, x_scales, d_words, d_scales, g
             for i, t in enumerate(slots):
                 nc.scalar.activation(dst[:, i, :], score[t], ACT.Relu, scale=g_abs[:, t : t + 1])
 
-        key_got = [tile_at(2 * H + S, [P, H], U32, "a_got"), tile([P, H], U32, "x_scale_got")]
+        key_got = [tile_at(2048, [P, H], U32, "a_got"), tile_at(4096, [P, H], U32, "b_got")]
         for got, key_list in zip(key_got, (k1_sb, k2_sb)):
             nc.vector.tensor_copy(got[:], d_word_tab[:].indirect(key_list[:]))
-        key_codes = [deal(tile([P, H], U32, name), got) for name, got in zip(("a_codes", "b_codes"), key_got)]
+        key_codes = [deal(tile([P, H], U32, "a_codes"), key_got[0])]
 
         def warm_up(bank_name, passes):
             warm_bank = ps.tile([WARM_ROWS, H], F32, name=bank_name)
@@ -170,10 +187,12 @@ def tile_picked_maxsim_relu_p_kernel(tc, x_words, x_scales, d_words, d_scales, g
 
         x_codes = []
         for h in range(2):
-            got = tile([P, HALF], U32, "x_codes%d" % h)
+            got = tile_at(8192 + 1024 * h, [P, HALF], U32, "x_codes%d" % h)
             nc.vector.tensor_copy(got[:], x_word_tab[:].indirect(offs_sb[:, 16 * h : 16 * (h + 1)]))
             x_codes.append(got)
-        w_codes, w_plane = quantise(tile([P, N], U32, "w_codes"), w_woven, "w_plane")
+            if h == 0:
+                key_codes.append(deal(tile_at(6144, [P, H], U32, "b_codes"), key_got[1]))
+        w_early_mx = quantise(tile([P, EARLY], U32, "w_codes"), w_woven, "w_plane")
 
         ra = [tile([P, SLOTS, HALF], BF16, "ra%d" % h) for h in range(2)]
         z = [tile([P, SLOTS, HALF], BF16, "z%d" % h) for h in range(2)]
@@ -191,6 +210,8 @@ def tile_picked_maxsim_relu_p_kernel(tc, x_words, x_scales, d_words, d_scales, g
         relu_out(rb, b_scores, range(2, SLOTS))
         warm_up("bank_a11", 1)
         best(1, 0, b_scores)
+        w_late_mx = quantise(tile([P, LATE], U32, "ra0"), w_late_woven, "w_late_plane")
+        w_mx = [[part[:, P * v : P * (v + 1)] for part in w_early_mx] for v in range(EARLY // P)] + [[part[:] for part in w_late_mx]]
 
         out_rows = out.rearrange("(v p) j -> v p j", p=P)
 
@@ -207,11 +228,10 @@ def tile_picked_maxsim_relu_p_kernel(tc, x_words, x_scales, d_words, d_scales, g
             banks = [ps.tile([P, 2, QUARTER], F32, name="bank_%s%d%d" % ("ab"[v // 2], h, v % 2)) for v in range(SLOTS)]
             for c in range(2):
                 for v in range(SLOTS):
-                    cols = slice(P * v, P * (v + 1))
                     nc.tensor.matmul_mx(
                         out=banks[v][:, c, :],
-                        lhsT=w_codes[:, cols].bitcast(FP8X4),
-                        lhsT_scale=w_plane[:, cols],
+                        lhsT=w_mx[v][0].bitcast(FP8X4),
+                        lhsT_scale=w_mx[v][1],
                         rhs=z_mx[c][0][:].bitcast(FP8X4),
                         rhs_scale=z_mx[c][1][:],
                         start=True,

@@ -247,4 +247,4 @@ def tile_picked_maxsim_relu_p_kernel(tc, x_words, x_scales, d_words, d_scales, g
         for c in range(2):
             cols = slice(QUARTER * c, QUARTER * (c + 1))
             nc.vector.tensor_tensor(z[1][:, 2:, cols], ra[1][:, 2:, cols], rb[:, :, cols], ALU.max)
-        values(1, weave_and_quantise(1), (nc.scalar.copy, nc.vector.tensor_copy) * 2, (nc.sync, nc.sync, nc.scalar, nc.sync))
+        values(1, weave_and_quantise(1), (nc.scalar.copy, nc.vector.tensor_copy) * 2, (nc.sync,) * 4)

@@ -1,7 +1,6 @@
 from contextlib import ExitStack
 
 import concourse.mybir as mybir
-from concourse.masks import make_identity
 
 F32 = mybir.dt.float32
 BF16 = mybir.dt.bfloat16
@@ -20,10 +19,10 @@ RUN = 8
 HALF = S // 2
 QUARTER = S // 4
 WARM_ROWS = 32
-W_RAW_AT = (0, 3328, 12288, 7936)
 EARLY = 384
 LATE = N - EARLY
-SCALE_GOT_AT = 14336
+SCALE_GOT_AT = 8192
+PLANES_AT = 10240
 SCORE_SCALE = 0.0625
 FLOPS = 2 * K * H * S * 2 + 2 * H * N * S
 
@@ -47,78 +46,59 @@ def tile_picked_maxsim_relu_p_kernel(tc, x_words, x_scales, d_words, d_scales, g
         d_scale_tab = tile([P, G], U8, "d_scale_tab")
         x_scale_tab = tile([P, T], U8, "x_scale_tab")
         d_word_tab = tile([P, G], U32, "d_word_tab")
-        x_word_tab = tile([P, T], U32, "x_word_tab")
-        gn_blocks = tile([P, SLOTS, RUN], F32, "gn_blocks")
-        identity = tile([P, P], F32, "identity")
-        w_raw = [tile_at(W_RAW_AT[t], [P, EARLY], F32, "w_raw%d" % t) for t in range(SLOTS)]
-
-        def load_scale_rows(tab, scales):
-            nc.sync.dma_start(tab[:].bitcast(I32)[0:P:RUN, :], scales[0].bitcast(I32))
+        x_word_tab = tile_at(0, [P, T], U32, "x_word_tab")
+        g = tile_at(PLANES_AT, [P, SLOTS], F32, "g")
+        w_raw = tile([P, SLOTS, EARLY], F32, "w_raw")
 
         def load_words(tab, words):
             nc.sync.dma_start(tab[:].bitcast(I32), words[0].rearrange("p n t -> p (n t)").bitcast(I32))
 
-        nc.vector.memset(d_scale_tab[:].bitcast(I32), 0)
-        nc.vector.memset(identity[:], 0.0)
         nc.vector.memset(x_scale_tab[:].bitcast(I32), 0)
-        w_rows = w1.rearrange("(b t r) m -> t b r m", t=SLOTS, r=RUN)
-        nc.sync.dma_start(w_raw[0][:], w_rows[0][:, :, 0:EARLY])
+        w_rows = w1.rearrange("(p t) m -> p t m", t=SLOTS)
         nc.sync.dma_start(k1_sb[:], k1)
-        nc.sync.dma_start(
-            gn_blocks[:].rearrange("p t r -> p (t r)"),
-            gn.rearrange("(b c) o -> b o c", c=SLOTS * RUN).to_broadcast([P // RUN, RUN, SLOTS * RUN]),
-        )
+        nc.sync.dma_start(d_scale_tab[:].bitcast(I32), d_scales[0].bitcast(I32).unsqueeze(1).to_broadcast([P // RUN, RUN, G // 4]))
         nc.sync.dma_start(k2_sb[:], k2)
-        load_scale_rows(d_scale_tab, d_scales)
-        for t in range(1, SLOTS):
-            nc.sync.dma_start(w_raw[t][:], w_rows[t][:, :, 0:EARLY])
         nc.sync.dma_start(offs_sb[:], offs)
-        load_scale_rows(x_scale_tab, x_scales)
+        nc.sync.dma_start(g[:], gn.rearrange("(p t) o -> p (t o)", t=SLOTS))
+        nc.sync.dma_start(x_scale_tab[:].bitcast(I32)[0:P:RUN, :], x_scales[0].bitcast(I32))
+        nc.sync.dma_start(w_raw[:], w_rows[:, :, 0:EARLY])
         load_words(d_word_tab, d_words)
         load_words(x_word_tab, x_words)
 
-        make_identity(nc, identity[:], nomemset=True)
-
-        own_place = identity[:]
-        while own_place.shape[1] > RUN:
-            width = own_place.shape[1] // 2
-            summed = tile([P, width], F32, "own_place%d" % width)
-            nc.gpsimd.tensor_tensor(summed[:], own_place[:, 0:width], own_place[:, width:], ALU.add)
-            own_place = summed[:]
-        gn_masked = tile([P, SLOTS, RUN], F32, "gn_masked")
-        nc.gpsimd.tensor_tensor(gn_masked[:], gn_blocks[:], own_place.unsqueeze(1).to_broadcast([P, SLOTS, RUN]), ALU.mult)
         g_abs = tile([P, SLOTS], F32, "g_abs")
         g_step = tile([P, SLOTS], F32, "g_step")
         g_sign = tile([P, SLOTS], F32, "g_sign")
-        summands = tile([P, 2, SLOTS, RUN], F32, "summands")
-        for t in range(SLOTS):
-            nc.scalar.activation(summands[:, 0, t, :], gn_masked[:, t, :], ACT.Sign, accum_out=g_step[:, t : t + 1])
+        nc.scalar.activation(g_step[:], g[:], ACT.Sign)
+        nc.scalar.activation(g_abs[:], g[:], ACT.Abs, scale=SCORE_SCALE)
         nc.scalar.activation(g_sign[:], g_step[:], ACT.Sign, bias=0.5)
 
         d_scale_got = tile([P, 2 * H], U8, "d_scale_got")
         x_scale_got = tile_at(SCALE_GOT_AT, [P, S], U8, "x_scale_got")
-        planes = tile_at(0, [P, 2 * H + S], U8, "planes")
+        planes = tile_at(PLANES_AT, [P, 2 * H + S], U8, "planes")
+
+        def deal_bytes(side):
+            cols = slice(H * side, H * (side + 1))
+            nc.vector.tensor_copy(
+                planes[:, cols].rearrange("p (t m) -> p m t", t=SLOTS),
+                d_scale_got[:, cols].rearrange("p (m t) -> p m t", t=SLOTS),
+            )
+
         nc.vector.tensor_copy(d_scale_got[:, 0:H], d_scale_tab[:].indirect(k1_sb[:]))
         nc.vector.tensor_copy(d_scale_got[:, H : 2 * H], d_scale_tab[:].indirect(k2_sb[:]))
         nc.vector.tensor_copy(x_scale_got[:], x_scale_tab[:].indirect(offs_sb[:]))
-        nc.vector.tensor_copy(
-            planes[:, 0 : 2 * H].bitcast(I32).rearrange("p (l t b w) -> p l t b w", l=2, t=SLOTS, w=2),
-            d_scale_got[:].bitcast(I32).rearrange("p (l b t w) -> p l t b w", l=2, t=SLOTS, w=2),
-        )
+        deal_bytes(0)
+        deal_bytes(1)
         nc.vector.tensor_copy(planes[:, 2 * H :].bitcast(I32), x_scale_got[:].bitcast(I32))
         for r in range(1, 4):
             nc.sync.dma_start(planes[:].bitcast(I32)[r:P:32, :], planes[:].bitcast(I32)[RUN * r : P : 32, :])
         w_late = tile_at(SCALE_GOT_AT, [P, SLOTS, LATE], F32, "w_late")
-        for t in range(SLOTS):
-            nc.sync.dma_start(w_late[:, t, :], w_rows[t][:, :, EARLY:])
+        nc.sync.dma_start(w_late[:], w_rows[:, :, EARLY:])
 
         w_signed = tile([P, SLOTS, EARLY], BF16, "w_signed")
         w_woven = tile([P, SLOTS * EARLY], BF16, "w_woven")
         for t in range(SLOTS):
-            nc.scalar.activation(w_signed[:, t, :], w_raw[t][:], ACT.Copy, scale=g_sign[:, t : t + 1])
+            nc.scalar.activation(w_signed[:, t, :], w_raw[:, t, :], ACT.Copy, scale=g_sign[:, t : t + 1])
         nc.scalar.copy(w_woven[:].rearrange("p (m t) -> p m t", t=SLOTS), w_signed[:].rearrange("p t m -> p m t"))
-        for t in range(SLOTS):
-            nc.scalar.activation(summands[:, 1, t, :], gn_masked[:, t, :], ACT.Abs, scale=SCORE_SCALE, accum_out=g_abs[:, t : t + 1])
 
         w_late_woven = tile([P, SLOTS * LATE], BF16, "w_late_woven")
         piece = LATE // 2
@@ -132,8 +112,8 @@ def tile_picked_maxsim_relu_p_kernel(tc, x_words, x_scales, d_words, d_scales, g
 
         def deal(codes, got):
             nc.vector.tensor_copy(
-                codes[:].bitcast(I32).rearrange("p (t b r) -> p t b r", t=SLOTS, r=RUN),
-                got[:].bitcast(I32).rearrange("p (b t r) -> p t b r", t=SLOTS, r=RUN),
+                codes[:].bitcast(I32).rearrange("p (t m) -> p m t", t=SLOTS),
+                got[:].bitcast(I32).rearrange("p (m t) -> p m t", t=SLOTS),
             )
             return codes
 
@@ -165,10 +145,10 @@ def tile_picked_maxsim_relu_p_kernel(tc, x_words, x_scales, d_words, d_scales, g
             for i, t in enumerate(slots):
                 nc.scalar.activation(dst[:, i, :], score[t], ACT.Relu, scale=g_abs[:, t : t + 1])
 
-        key_got = [tile_at(2048, [P, H], U32, "a_got"), tile_at(4096, [P, H], U32, "b_got")]
+        key_got = [tile([P, H], U32, "a_got"), tile([P, H], U32, "b_got")]
         for got, key_list in zip(key_got, (k1_sb, k2_sb)):
             nc.vector.tensor_copy(got[:], d_word_tab[:].indirect(key_list[:]))
-        key_codes = [deal(tile([P, H], U32, "a_codes"), key_got[0])]
+        key_codes = [deal(tile([P, H], U32, "ab"[side] + "_codes"), key_got[side]) for side in range(2)]
 
         def warm_up(bank_name, passes):
             warm_bank = ps.tile([WARM_ROWS, H], F32, name=bank_name)
@@ -187,12 +167,10 @@ def tile_picked_maxsim_relu_p_kernel(tc, x_words, x_scales, d_words, d_scales, g
 
         x_codes = []
         for h in range(2):
-            got = tile_at(8192 + 1024 * h, [P, HALF], U32, "x_codes%d" % h)
+            got = tile([P, HALF], U32, "x_codes%d" % h)
             nc.vector.tensor_copy(got[:], x_word_tab[:].indirect(offs_sb[:, 16 * h : 16 * (h + 1)]))
             x_codes.append(got)
-            if h == 0:
-                key_codes.append(deal(tile_at(6144, [P, H], U32, "b_codes"), key_got[1]))
-        w_early_mx = quantise(tile([P, EARLY], U32, "w_codes"), w_woven, "w_plane")
+        w_early_mx = quantise(tile_at(0, [P, EARLY], U32, "w_codes"), w_woven, "w_plane")
 
         ra = [tile([P, SLOTS, HALF], BF16, "ra%d" % h) for h in range(2)]
         z = [tile([P, SLOTS, HALF], BF16, "z%d" % h) for h in range(2)]

@@ -19,10 +19,8 @@ RUN = 8
 HALF = S // 2
 QUARTER = S // 4
 WARM_ROWS = 32
-EARLY = 384
-LATE = N - EARLY
-SCALE_GOT_AT = 8192
-PLANES_AT = 10240
+W_PART = N // 2
+PLANES_AT = 0
 SCORE_SCALE = 0.0625
 FLOPS = 2 * K * H * S * 2 + 2 * H * N * S
 
@@ -46,9 +44,9 @@ def tile_picked_maxsim_relu_p_kernel(tc, x_words, x_scales, d_words, d_scales, g
         d_scale_tab = tile([P, G], U8, "d_scale_tab")
         x_scale_tab = tile([P, T], U8, "x_scale_tab")
         d_word_tab = tile([P, G], U32, "d_word_tab")
-        x_word_tab = tile_at(0, [P, T], U32, "x_word_tab")
+        x_word_tab = tile([P, T], U32, "x_word_tab")
         g = tile_at(PLANES_AT, [P, SLOTS], F32, "g")
-        w_raw = tile([P, SLOTS, EARLY], F32, "w_raw")
+        w_raw = [tile([P, SLOTS, W_PART], F32, "w_raw%d" % u) for u in range(2)]
 
         def load_words(tab, words):
             nc.sync.dma_start(tab[:].bitcast(I32), words[0].rearrange("p n t -> p (n t)").bitcast(I32))
@@ -61,8 +59,9 @@ def tile_picked_maxsim_relu_p_kernel(tc, x_words, x_scales, d_words, d_scales, g
         nc.sync.dma_start(offs_sb[:], offs)
         nc.sync.dma_start(g[:], gn.rearrange("(p t) o -> p (t o)", t=SLOTS))
         nc.sync.dma_start(x_scale_tab[:].bitcast(I32)[0:P:RUN, :], x_scales[0].bitcast(I32))
-        nc.sync.dma_start(w_raw[:], w_rows[:, :, 0:EARLY])
+        nc.sync.dma_start(w_raw[0][:], w_rows[:, :, 0:W_PART])
         load_words(d_word_tab, d_words)
+        nc.sync.dma_start(w_raw[1][:], w_rows[:, :, W_PART:])
         load_words(x_word_tab, x_words)
 
         g_abs = tile([P, SLOTS], F32, "g_abs")
@@ -73,7 +72,7 @@ def tile_picked_maxsim_relu_p_kernel(tc, x_words, x_scales, d_words, d_scales, g
         nc.scalar.activation(g_sign[:], g_step[:], ACT.Sign, bias=0.5)
 
         d_scale_got = tile([P, 2 * H], U8, "d_scale_got")
-        x_scale_got = tile_at(SCALE_GOT_AT, [P, S], U8, "x_scale_got")
+        x_scale_got = tile([P, S], U8, "x_scale_got")
         planes = tile_at(PLANES_AT, [P, 2 * H + S], U8, "planes")
 
         def deal_bytes(side):
@@ -91,23 +90,15 @@ def tile_picked_maxsim_relu_p_kernel(tc, x_words, x_scales, d_words, d_scales, g
         nc.vector.tensor_copy(planes[:, 2 * H :].bitcast(I32), x_scale_got[:].bitcast(I32))
         for r in range(1, 4):
             nc.sync.dma_start(planes[:].bitcast(I32)[r:P:32, :], planes[:].bitcast(I32)[RUN * r : P : 32, :])
-        w_late = tile_at(SCALE_GOT_AT, [P, SLOTS, LATE], F32, "w_late")
-        nc.sync.dma_start(w_late[:], w_rows[:, :, EARLY:])
 
-        w_signed = tile([P, SLOTS, EARLY], BF16, "w_signed")
-        w_woven = tile([P, SLOTS * EARLY], BF16, "w_woven")
-        for t in range(SLOTS):
-            nc.scalar.activation(w_signed[:, t, :], w_raw[:, t, :], ACT.Copy, scale=g_sign[:, t : t + 1])
-        nc.scalar.copy(w_woven[:].rearrange("p (m t) -> p m t", t=SLOTS), w_signed[:].rearrange("p t m -> p m t"))
-
-        w_late_woven = tile([P, SLOTS * LATE], BF16, "w_late_woven")
-        piece = LATE // 2
-        for c in range(2):
-            nc.gpsimd.tensor_tensor(
-                w_late_woven[:].rearrange("p (m t) -> p m t", t=SLOTS)[:, piece * c : piece * (c + 1), :],
-                w_late[:, :, piece * c : piece * (c + 1)].rearrange("p t m -> p m t"),
-                g_sign[:].unsqueeze(1).to_broadcast([P, piece, SLOTS]),
-                ALU.mult,
+        w_woven = tile([P, SLOTS * N], BF16, "w_woven")
+        for u in range(2):
+            w_signed = tile([P, SLOTS, W_PART], BF16, "w_signed%d" % u)
+            for t in range(SLOTS):
+                nc.scalar.activation(w_signed[:, t, :], w_raw[u][:, t, :], ACT.Copy, scale=g_sign[:, t : t + 1])
+            nc.scalar.copy(
+                w_woven[:, SLOTS * W_PART * u : SLOTS * W_PART * (u + 1)].rearrange("p (m t) -> p m t", t=SLOTS),
+                w_signed[:].rearrange("p t m -> p m t"),
             )
 
         def deal(codes, got):
@@ -170,7 +161,8 @@ def tile_picked_maxsim_relu_p_kernel(tc, x_words, x_scales, d_words, d_scales, g
             got = tile([P, HALF], U32, "x_codes%d" % h)
             nc.vector.tensor_copy(got[:], x_word_tab[:].indirect(offs_sb[:, 16 * h : 16 * (h + 1)]))
             x_codes.append(got)
-        w_early_mx = quantise(tile_at(0, [P, EARLY], U32, "w_codes"), w_woven, "w_plane")
+        w_all = quantise(tile([P, N], U32, "w_codes"), w_woven, "w_plane")
+        w_mx = [[part[:, P * v : P * (v + 1)] for part in w_all] for v in range(SLOTS)]
 
         ra = [tile([P, SLOTS, HALF], BF16, "ra%d" % h) for h in range(2)]
         z = [tile([P, SLOTS, HALF], BF16, "z%d" % h) for h in range(2)]
@@ -188,8 +180,6 @@ def tile_picked_maxsim_relu_p_kernel(tc, x_words, x_scales, d_words, d_scales, g
         relu_out(rb, b_scores, range(2, SLOTS))
         warm_up("bank_a11", 1)
         best(1, 0, b_scores)
-        w_late_mx = quantise(tile([P, LATE], U32, "ra0"), w_late_woven, "w_late_plane")
-        w_mx = [[part[:, P * v : P * (v + 1)] for part in w_early_mx] for v in range(EARLY // P)] + [[part[:] for part in w_late_mx]]
 
         out_rows = out.rearrange("(v p) j -> v p j", p=P)
 

@@ -45,21 +45,25 @@ def tile_picked_maxsim_relu_p_kernel(tc, x_words, x_scales, d_words, d_scales, g
         x_scale_tab = tile([P, T], U8, "x_scale_tab")
         d_word_tab = tile([P, G], U32, "d_word_tab")
         x_word_tab = tile([P, T], U32, "x_word_tab")
-        g = tile_at(PLANES_AT, [P, SLOTS], F32, "g")
-        w_raw = [tile([P, SLOTS, W_PART], F32, "w_raw%d" % u) for u in range(2)]
+        g = tile([P, SLOTS], F32, "g")
+        w_raw = [tile_at(PLANES_AT, [P, SLOTS, W_PART], F32, "w_raw0"), tile([P, SLOTS, W_PART], F32, "w_raw1")]
 
         def load_words(tab, words):
             nc.sync.dma_start(tab[:].bitcast(I32), words[0].rearrange("p n t -> p (n t)").bitcast(I32))
 
+        def load_scale_rows(tab, scales):
+            nc.sync.dma_start(tab[:].bitcast(I32)[0:P:RUN, :], scales[0].bitcast(I32))
+
+        nc.vector.memset(d_scale_tab[:].bitcast(I32), 0)
         nc.vector.memset(x_scale_tab[:].bitcast(I32), 0)
         w_rows = w1.rearrange("(p t) m -> p t m", t=SLOTS)
         nc.sync.dma_start(k1_sb[:], k1)
-        nc.sync.dma_start(d_scale_tab[:].bitcast(I32), d_scales[0].bitcast(I32).unsqueeze(1).to_broadcast([P // RUN, RUN, G // 4]))
         nc.sync.dma_start(k2_sb[:], k2)
-        nc.sync.dma_start(offs_sb[:], offs)
         nc.sync.dma_start(g[:], gn.rearrange("(p t) o -> p (t o)", t=SLOTS))
-        nc.sync.dma_start(x_scale_tab[:].bitcast(I32)[0:P:RUN, :], x_scales[0].bitcast(I32))
+        nc.sync.dma_start(offs_sb[:], offs)
+        load_scale_rows(d_scale_tab, d_scales)
         nc.sync.dma_start(w_raw[0][:], w_rows[:, :, 0:W_PART])
+        load_scale_rows(x_scale_tab, x_scales)
         load_words(d_word_tab, d_words)
         nc.sync.dma_start(w_raw[1][:], w_rows[:, :, W_PART:])
         load_words(x_word_tab, x_words)

@@ -19,7 +19,6 @@ RUN = 8
 HALF = S // 2
 QUARTER = S // 4
 WARM_ROWS = 32
-W_PART = N // 2
 PLANES_AT = 0
 SCORE_SCALE = 0.0625
 FLOPS = 2 * K * H * S * 2 + 2 * H * N * S
@@ -46,7 +45,8 @@ def tile_picked_maxsim_relu_p_kernel(tc, x_words, x_scales, d_words, d_scales, g
         d_word_tab = tile([P, G], U32, "d_word_tab")
         x_word_tab = tile([P, T], U32, "x_word_tab")
         g = tile([P, SLOTS], F32, "g")
-        w_raw = [tile_at(PLANES_AT, [P, SLOTS, W_PART], F32, "w_raw0"), tile([P, SLOTS, W_PART], F32, "w_raw1")]
+        w_first = tile_at(PLANES_AT, [P, 2, N], F32, "w_first")
+        w_last = [tile([P, N], F32, "w_last%d" % t) for t in range(2, SLOTS)]
 
         def load_words(tab, words):
             nc.sync.dma_start(tab[:].bitcast(I32), words[0].rearrange("p n t -> p (n t)").bitcast(I32))
@@ -62,10 +62,11 @@ def tile_picked_maxsim_relu_p_kernel(tc, x_words, x_scales, d_words, d_scales, g
         nc.sync.dma_start(g[:], gn.rearrange("(p t) o -> p (t o)", t=SLOTS))
         nc.sync.dma_start(offs_sb[:], offs)
         load_scale_rows(d_scale_tab, d_scales)
-        nc.sync.dma_start(w_raw[0][:], w_rows[:, :, 0:W_PART])
+        nc.sync.dma_start(w_first[:], w_rows[:, 0:2, :])
         load_scale_rows(x_scale_tab, x_scales)
         load_words(d_word_tab, d_words)
-        nc.sync.dma_start(w_raw[1][:], w_rows[:, :, W_PART:])
+        for t in range(2, SLOTS):
+            nc.sync.dma_start(w_last[t - 2][:], w_rows[:, t, :])
         load_words(x_word_tab, x_words)
 
         g_abs = tile([P, SLOTS], F32, "g_abs")
@@ -79,31 +80,22 @@ def tile_picked_maxsim_relu_p_kernel(tc, x_words, x_scales, d_words, d_scales, g
         x_scale_got = tile([P, S], U8, "x_scale_got")
         planes = tile_at(PLANES_AT, [P, 2 * H + S], U8, "planes")
 
-        def deal_bytes(side):
-            cols = slice(H * side, H * (side + 1))
-            nc.vector.tensor_copy(
-                planes[:, cols].rearrange("p (t m) -> p m t", t=SLOTS),
-                d_scale_got[:, cols].rearrange("p (m t) -> p m t", t=SLOTS),
-            )
-
         nc.vector.tensor_copy(d_scale_got[:, 0:H], d_scale_tab[:].indirect(k1_sb[:]))
         nc.vector.tensor_copy(d_scale_got[:, H : 2 * H], d_scale_tab[:].indirect(k2_sb[:]))
         nc.vector.tensor_copy(x_scale_got[:], x_scale_tab[:].indirect(offs_sb[:]))
-        deal_bytes(0)
-        deal_bytes(1)
+        nc.vector.tensor_copy(
+            planes[:, 0 : 2 * H].rearrange("p (l t m) -> p l t m", l=2, t=SLOTS),
+            d_scale_got[:].rearrange("p (l m t) -> p l t m", l=2, t=SLOTS),
+        )
         nc.vector.tensor_copy(planes[:, 2 * H :].bitcast(I32), x_scale_got[:].bitcast(I32))
         for r in range(1, 4):
             nc.sync.dma_start(planes[:].bitcast(I32)[r:P:32, :], planes[:].bitcast(I32)[RUN * r : P : 32, :])
 
         w_woven = tile([P, SLOTS * N], BF16, "w_woven")
-        for u in range(2):
-            w_signed = tile([P, SLOTS, W_PART], BF16, "w_signed%d" % u)
-            for t in range(SLOTS):
-                nc.scalar.activation(w_signed[:, t, :], w_raw[u][:, t, :], ACT.Copy, scale=g_sign[:, t : t + 1])
-            nc.scalar.copy(
-                w_woven[:, SLOTS * W_PART * u : SLOTS * W_PART * (u + 1)].rearrange("p (m t) -> p m t", t=SLOTS),
-                w_signed[:].rearrange("p t m -> p m t"),
-            )
+        w_signed = tile([P, SLOTS, N], BF16, "w_signed")
+        for t, rows in enumerate([w_first[:, 0, :], w_first[:, 1, :], w_last[0][:], w_last[1][:]]):
+            nc.scalar.activation(w_signed[:, t, :], rows, ACT.Copy, scale=g_sign[:, t : t + 1])
+        nc.scalar.copy(w_woven[:].rearrange("p (m t) -> p m t", t=SLOTS), w_signed[:].rearrange("p t m -> p m t"))
 
         def deal(codes, got):
             nc.vector.tensor_copy(

@@ -20,6 +20,7 @@ HALF = S // 2
 QUARTER = S // 4
 WARM_ROWS = 32
 PLANES_AT = 0
+W_HEAD = 384
 SCORE_SCALE = 0.0625
 FLOPS = 2 * K * H * S * 2 + 2 * H * N * S
 
@@ -44,8 +45,9 @@ def tile_picked_maxsim_relu_p_kernel(tc, x_words, x_scales, d_words, d_scales, g
         x_scale_tab = tile([P, T], U8, "x_scale_tab")
         d_word_tab = tile([P, G], U32, "d_word_tab")
         x_word_tab = tile([P, T], U32, "x_word_tab")
-        g = tile([P, SLOTS], F32, "g")
-        w_first = tile_at(PLANES_AT, [P, 2, N], F32, "w_first")
+        g = tile_at(PLANES_AT, [P, SLOTS], F32, "g")
+        w_head = tile([P, W_HEAD], F32, "w_head")
+        w_next = tile([P, 2 * N - W_HEAD], F32, "w_next")
         w_last = [tile([P, N], F32, "w_last%d" % t) for t in range(2, SLOTS)]
 
         def load_words(tab, words):
@@ -57,14 +59,16 @@ def tile_picked_maxsim_relu_p_kernel(tc, x_words, x_scales, d_words, d_scales, g
         nc.vector.memset(d_scale_tab[:].bitcast(I32), 0)
         nc.vector.memset(x_scale_tab[:].bitcast(I32), 0)
         w_rows = w1.rearrange("(p t) m -> p t m", t=SLOTS)
+        w_flat = w1.rearrange("(p t) m -> p (t m)", t=SLOTS)
+        nc.sync.dma_start(w_head[:], w_flat[:, 0:W_HEAD])
         nc.sync.dma_start(k1_sb[:], k1)
         nc.sync.dma_start(k2_sb[:], k2)
-        nc.sync.dma_start(g[:], gn.rearrange("(p t) o -> p (t o)", t=SLOTS))
-        nc.sync.dma_start(offs_sb[:], offs)
         load_scale_rows(d_scale_tab, d_scales)
-        nc.sync.dma_start(w_first[:], w_rows[:, 0:2, :])
+        nc.sync.dma_start(offs_sb[:], offs)
+        nc.sync.dma_start(g[:], gn.rearrange("(p t) o -> p (t o)", t=SLOTS))
         load_scale_rows(x_scale_tab, x_scales)
         load_words(d_word_tab, d_words)
+        nc.sync.dma_start(w_next[:], w_flat[:, W_HEAD : 2 * N])
         for t in range(2, SLOTS):
             nc.sync.dma_start(w_last[t - 2][:], w_rows[:, t, :])
         load_words(x_word_tab, x_words)
@@ -93,8 +97,15 @@ def tile_picked_maxsim_relu_p_kernel(tc, x_words, x_scales, d_words, d_scales, g
 
         w_woven = tile([P, SLOTS * N], BF16, "w_woven")
         w_signed = tile([P, SLOTS, N], BF16, "w_signed")
-        for t, rows in enumerate([w_first[:, 0, :], w_first[:, 1, :], w_last[0][:], w_last[1][:]]):
-            nc.scalar.activation(w_signed[:, t, :], rows, ACT.Copy, scale=g_sign[:, t : t + 1])
+        parts = [
+            (0, 0, w_head[:]),
+            (0, W_HEAD, w_next[:, 0 : N - W_HEAD]),
+            (1, 0, w_next[:, N - W_HEAD :]),
+            (2, 0, w_last[0][:]),
+            (3, 0, w_last[1][:]),
+        ]
+        for t, first, rows in parts:
+            nc.scalar.activation(w_signed[:, t, first : first + rows.shape[1]], rows, ACT.Copy, scale=g_sign[:, t : t + 1])
         nc.scalar.copy(w_woven[:].rearrange("p (m t) -> p m t", t=SLOTS), w_signed[:].rearrange("p t m -> p m t"))
 
         def deal(codes, got):

@@ -19,7 +19,10 @@ RUN = 8
 HALF = S // 2
 QUARTER = S // 4
 WARM_ROWS = 32
-PLANES_AT = 0
+DEALT_AT = 4096
+B_CODES_AT = 2112
+X_LAST_AT = 4160
+W_CODES_AT = 5184
 W_HEAD = 384
 SCORE_SCALE = 0.0625
 FLOPS = 2 * K * H * S * 2 + 2 * H * N * S
@@ -45,7 +48,7 @@ def tile_picked_maxsim_relu_p_kernel(tc, x_words, x_scales, d_words, d_scales, g
         x_scale_tab = tile([P, T], U8, "x_scale_tab")
         d_word_tab = tile([P, G], U32, "d_word_tab")
         x_word_tab = tile([P, T], U32, "x_word_tab")
-        g = tile_at(PLANES_AT, [P, SLOTS], F32, "g")
+        g = tile_at(DEALT_AT, [P, SLOTS], F32, "g")
         w_head = tile([P, W_HEAD], F32, "w_head")
         w_next = tile([P, 2 * N - W_HEAD], F32, "w_next")
         w_last = [tile([P, N], F32, "w_last%d" % t) for t in range(2, SLOTS)]
@@ -58,6 +61,8 @@ def tile_picked_maxsim_relu_p_kernel(tc, x_words, x_scales, d_words, d_scales, g
 
         nc.vector.memset(d_scale_tab[:].bitcast(I32), 0)
         nc.vector.memset(x_scale_tab[:].bitcast(I32), 0)
+        planes = tile([P, 2 * H + S], U8, "planes")
+        nc.vector.memset(planes[:].bitcast(I32), 0)
         w_rows = w1.rearrange("(p t) m -> p t m", t=SLOTS)
         w_flat = w1.rearrange("(p t) m -> p (t m)", t=SLOTS)
         nc.sync.dma_start(w_head[:], w_flat[:, 0:W_HEAD])
@@ -82,18 +87,18 @@ def tile_picked_maxsim_relu_p_kernel(tc, x_words, x_scales, d_words, d_scales, g
 
         d_scale_got = tile([P, 2 * H], U8, "d_scale_got")
         x_scale_got = tile([P, S], U8, "x_scale_got")
-        planes = tile_at(PLANES_AT, [P, 2 * H + S], U8, "planes")
+        dealt = tile_at(DEALT_AT, [P, 2 * H + S], U8, "dealt")
 
         nc.vector.tensor_copy(d_scale_got[:, 0:H], d_scale_tab[:].indirect(k1_sb[:]))
         nc.vector.tensor_copy(d_scale_got[:, H : 2 * H], d_scale_tab[:].indirect(k2_sb[:]))
         nc.vector.tensor_copy(x_scale_got[:], x_scale_tab[:].indirect(offs_sb[:]))
         nc.vector.tensor_copy(
-            planes[:, 0 : 2 * H].rearrange("p (l t m) -> p l t m", l=2, t=SLOTS),
+            dealt[:, 0 : 2 * H].rearrange("p (l t m) -> p l t m", l=2, t=SLOTS),
             d_scale_got[:].rearrange("p (l m t) -> p l t m", l=2, t=SLOTS),
         )
-        nc.vector.tensor_copy(planes[:, 2 * H :].bitcast(I32), x_scale_got[:].bitcast(I32))
-        for r in range(1, 4):
-            nc.sync.dma_start(planes[:].bitcast(I32)[r:P:32, :], planes[:].bitcast(I32)[RUN * r : P : 32, :])
+        nc.vector.tensor_copy(dealt[:, 2 * H :].bitcast(I32), x_scale_got[:].bitcast(I32))
+        for r in range(4):
+            nc.sync.dma_start(planes[:].bitcast(I32)[r:P:32, :], dealt[:].bitcast(I32)[RUN * r : P : 32, :])
 
         w_woven = tile([P, SLOTS * N], BF16, "w_woven")
         w_signed = tile([P, SLOTS, N], BF16, "w_signed")
@@ -146,7 +151,7 @@ def tile_picked_maxsim_relu_p_kernel(tc, x_words, x_scales, d_words, d_scales, g
         key_got = [tile([P, H], U32, "a_got"), tile([P, H], U32, "b_got")]
         for got, key_list in zip(key_got, (k1_sb, k2_sb)):
             nc.vector.tensor_copy(got[:], d_word_tab[:].indirect(key_list[:]))
-        key_codes = [deal(tile([P, H], U32, "ab"[side] + "_codes"), key_got[side]) for side in range(2)]
+        key_codes = [deal(tile([P, H], U32, "a_codes"), key_got[0])]
 
         def warm_up(bank_name, passes):
             warm_bank = ps.tile([WARM_ROWS, H], F32, name=bank_name)
@@ -165,10 +170,12 @@ def tile_picked_maxsim_relu_p_kernel(tc, x_words, x_scales, d_words, d_scales, g
 
         x_codes = []
         for h in range(2):
-            got = tile([P, HALF], U32, "x_codes%d" % h)
+            got = tile_at(X_LAST_AT, [P, HALF], U32, "x_codes1") if h else tile([P, HALF], U32, "x_codes0")
             nc.vector.tensor_copy(got[:], x_word_tab[:].indirect(offs_sb[:, 16 * h : 16 * (h + 1)]))
             x_codes.append(got)
-        w_all = quantise(tile([P, N], U32, "w_codes"), w_woven, "w_plane")
+            if h == 0:
+                key_codes.append(deal(tile_at(B_CODES_AT, [P, H], U32, "b_codes"), key_got[1]))
+        w_all = quantise(tile_at(W_CODES_AT, [P, N], U32, "w_codes"), w_woven, "w_plane")
         w_mx = [[part[:, P * v : P * (v + 1)] for part in w_all] for v in range(SLOTS)]
 
         ra = [tile([P, SLOTS, HALF], BF16, "ra%d" % h) for h in range(2)]

@@ -36,7 +36,7 @@ def tile_picked_maxsim_relu_p_kernel(tc, x_words, x_scales, d_words, d_scales, g
         reuse = ctx.enter_context(tc.tile_pool(name="reuse", bufs=1))
 
         def tile(shape, dtype, name):
-            return sb.tile(shape, dtype, name=name, align_bytes=64)
+            return sb.tile(shape, dtype, name=name, align_bytes=256)
 
         def tile_at(offset, shape, dtype, name):
             return reuse.tile(shape, dtype, name=name, align_bytes=64, offset=offset)

@@ -23,7 +23,8 @@ DEALT_AT = 4096
 B_CODES_AT = 2112
 X_LAST_AT = 4160
 W_CODES_AT = 5184
-W_HEAD = 384
+W_HEAD = 448
+W_TAIL = 128
 SCORE_SCALE = 0.0625
 FLOPS = 2 * K * H * S * 2 + 2 * H * N * S
 
@@ -51,7 +52,9 @@ def tile_picked_maxsim_relu_p_kernel(tc, x_words, x_scales, d_words, d_scales, g
         g = tile_at(DEALT_AT, [P, SLOTS], F32, "g")
         w_head = tile([P, W_HEAD], F32, "w_head")
         w_next = tile([P, 2 * N - W_HEAD], F32, "w_next")
-        w_last = [tile([P, N], F32, "w_last%d" % t) for t in range(2, SLOTS)]
+        w_third = tile([P, N], F32, "w_third")
+        w_last = tile([P, N - W_TAIL], F32, "w_last")
+        w_tail = tile([P, W_TAIL], F32, "w_tail")
 
         def load_words(tab, words):
             nc.sync.dma_start(tab[:].bitcast(I32), words[0].rearrange("p n t -> p (n t)").bitcast(I32))
@@ -74,9 +77,10 @@ def tile_picked_maxsim_relu_p_kernel(tc, x_words, x_scales, d_words, d_scales, g
         load_scale_rows(x_scale_tab, x_scales)
         load_words(d_word_tab, d_words)
         nc.sync.dma_start(w_next[:], w_flat[:, W_HEAD : 2 * N])
-        for t in range(2, SLOTS):
-            nc.sync.dma_start(w_last[t - 2][:], w_rows[:, t, :])
+        nc.sync.dma_start(w_third[:], w_rows[:, 2, :])
+        nc.sync.dma_start(w_last[:], w_rows[:, 3, 0 : N - W_TAIL])
         load_words(x_word_tab, x_words)
+        nc.sync.dma_start(w_tail[:], w_rows[:, 3, N - W_TAIL :])
 
         g_abs = tile([P, SLOTS], F32, "g_abs")
         g_step = tile([P, SLOTS], F32, "g_step")
@@ -106,12 +110,23 @@ def tile_picked_maxsim_relu_p_kernel(tc, x_words, x_scales, d_words, d_scales, g
             (0, 0, w_head[:]),
             (0, W_HEAD, w_next[:, 0 : N - W_HEAD]),
             (1, 0, w_next[:, N - W_HEAD :]),
-            (2, 0, w_last[0][:]),
-            (3, 0, w_last[1][:]),
+            (2, 0, w_third[:]),
+            (3, 0, w_last[:]),
         ]
-        for t, first, rows in parts:
+
+        def sign(t, first, rows):
             nc.scalar.activation(w_signed[:, t, first : first + rows.shape[1]], rows, ACT.Copy, scale=g_sign[:, t : t + 1])
-        nc.scalar.copy(w_woven[:].rearrange("p (m t) -> p m t", t=SLOTS), w_signed[:].rearrange("p t m -> p m t"))
+
+        def weave_w(cols):
+            nc.scalar.copy(
+                w_woven[:].rearrange("p (m t) -> p m t", t=SLOTS)[:, cols, :], w_signed[:].rearrange("p t m -> p m t")[:, cols, :]
+            )
+
+        for part in parts:
+            sign(*part)
+        weave_w(slice(0, N - W_TAIL))
+        sign(SLOTS - 1, N - W_TAIL, w_tail[:])
+        weave_w(slice(N - W_TAIL, N))
 
         def deal(codes, got):
             nc.vector.tensor_copy(
@@ -195,7 +210,7 @@ def tile_picked_maxsim_relu_p_kernel(tc, x_words, x_scales, d_words, d_scales, g
         warm_up("bank_a11", 1)
         best(1, 0, b_scores)
 
-        out_rows = out.rearrange("(v p) j -> v p j", p=P)
+        out_rows = out.rearrange("(v p) j -> p v j", p=P)
 
         def weave_and_quantise(h):
             woven = [tile([P, QUARTER * SLOTS], BF16, "z_woven%d%d" % (h, c)) for c in range(2)]
@@ -206,7 +221,7 @@ def tile_picked_maxsim_relu_p_kernel(tc, x_words, x_scales, d_words, d_scales, g
                 )
             return [quantise(tile([P, QUARTER], U32, "z_codes%d%d" % (h, c)), woven[c], "z_plane%d%d" % (h, c)) for c in range(2)]
 
-        def values(h, z_mx, copies, queues):
+        def values(h, z_mx, copies, stores):
             banks = [ps.tile([P, 2, QUARTER], F32, name="bank_%s%d%d" % ("ab"[v // 2], h, v % 2)) for v in range(SLOTS)]
             for c in range(2):
                 for v in range(SLOTS):
@@ -219,14 +234,15 @@ def tile_picked_maxsim_relu_p_kernel(tc, x_words, x_scales, d_words, d_scales, g
                         start=True,
                         stop=True,
                     )
-            for v in range(SLOTS):
-                res = tile([P, HALF], F32, "res%d%d" % (h, v))
-                copies[v](res[:], banks[v][:].rearrange("p c j -> p (c j)"))
-                queues[v].dma_start(out_rows[v][:, HALF * h : HALF * (h + 1)], res[:])
+            for blocks in stores:
+                res = tile([P, len(blocks), HALF], F32, "res%d%d" % (h, blocks[0]))
+                for u, v in enumerate(blocks):
+                    copies[v](res[:, u, :], banks[v][:].rearrange("p c j -> p (c j)"))
+                nc.sync.dma_start(out_rows[:, blocks[0] : blocks[-1] + 1, HALF * h : HALF * (h + 1)], res[:])
 
-        values(0, weave_and_quantise(0), (nc.scalar.copy,) * 4, (nc.sync,) * 4)
+        values(0, weave_and_quantise(0), (nc.scalar.copy,) * 4, [[0, 1], [2], [3]])
         best(1, 1, b_scores)
         for c in range(2):
             cols = slice(QUARTER * c, QUARTER * (c + 1))
             nc.vector.tensor_tensor(z[1][:, 2:, cols], ra[1][:, 2:, cols], rb[:, :, cols], ALU.max)
-        values(1, weave_and_quantise(1), (nc.scalar.copy, nc.vector.tensor_copy) * 2, (nc.sync,) * 4)
+        values(1, weave_and_quantise(1), (nc.scalar.copy, nc.vector.tensor_copy) * 2, [[0], [1], [2], [3]])

from contextlib import ExitStack

import concourse.mybir as mybir

F32 = mybir.dt.float32
BF16 = mybir.dt.bfloat16
I32 = mybir.dt.int32
U32 = mybir.dt.uint32
U16 = mybir.dt.uint16
U8 = mybir.dt.uint8
FP8X4 = mybir.dt.float8_e4m3fn_x4
ALU = mybir.AluOpType
ACT = mybir.ActivationFunctionType

P = 128
K, T, S, N, G, H = 512, 2048, 512, 512, 2048, 512
SLOTS = 4
RUN = 8
HALF = S // 2
QUARTER = S // 4
WARM_ROWS = 32
DEALT_AT = 4096
B_CODES_AT = 2112
X_LAST_AT = 4160
W_CODES_AT = 5184
W_HEAD = 448
W_TAIL = 128
SCORE_SCALE = 0.0625
FLOPS = 2 * K * H * S * 2 + 2 * H * N * S


def tile_picked_maxsim_relu_p_kernel(tc, x_words, x_scales, d_words, d_scales, gn, w1, offs, k1, k2, out):
    nc = tc.nc
    with ExitStack() as ctx:
        sb = ctx.enter_context(tc.tile_pool(name="sb", bufs=1))
        ps = ctx.enter_context(tc.psum_pool(name="ps", bufs=1))
        reuse = ctx.enter_context(tc.tile_pool(name="reuse", bufs=1))

        def tile(shape, dtype, name):
            return sb.tile(shape, dtype, name=name, align_bytes=256)

        def tile_at(offset, shape, dtype, name):
            return reuse.tile(shape, dtype, name=name, align_bytes=64, offset=offset)

        k1_sb = tile([P, H // 16], U16, "k1_sb")
        k2_sb = tile([P, H // 16], U16, "k2_sb")
        offs_sb = tile([P, S // 16], U16, "offs_sb")
        d_scale_tab = tile([P, G], U8, "d_scale_tab")
        x_scale_tab = tile([P, T], U8, "x_scale_tab")
        d_word_tab = tile([P, G], U32, "d_word_tab")
        x_word_tab = tile([P, T], U32, "x_word_tab")
        g = tile_at(DEALT_AT, [P, SLOTS], F32, "g")
        w_head = tile([P, W_HEAD], F32, "w_head")
        w_next = tile([P, 2 * N - W_HEAD], F32, "w_next")
        w_third = tile([P, N], F32, "w_third")
        w_last = tile([P, N - W_TAIL], F32, "w_last")
        w_tail = tile([P, W_TAIL], F32, "w_tail")

        def load_words(tab, words):
            nc.sync.dma_start(tab[:].bitcast(I32), words[0].rearrange("p n t -> p (n t)").bitcast(I32))

        def load_scale_rows(tab, scales):
            nc.sync.dma_start(tab[:].bitcast(I32)[0:P:RUN, :], scales[0].bitcast(I32))

        nc.vector.memset(d_scale_tab[:].bitcast(I32), 0)
        nc.vector.memset(x_scale_tab[:].bitcast(I32), 0)
        planes = tile([P, 2 * H + S], U8, "planes")
        nc.vector.memset(planes[:].bitcast(I32), 0)
        w_rows = w1.rearrange("(p t) m -> p t m", t=SLOTS)
        w_flat = w1.rearrange("(p t) m -> p (t m)", t=SLOTS)
        nc.sync.dma_start(w_head[:], w_flat[:, 0:W_HEAD])
        nc.sync.dma_start(k1_sb[:], k1)
        nc.sync.dma_start(k2_sb[:], k2)
        load_scale_rows(d_scale_tab, d_scales)
        nc.sync.dma_start(offs_sb[:], offs)
        nc.sync.dma_start(g[:], gn.rearrange("(p t) o -> p (t o)", t=SLOTS))
        load_scale_rows(x_scale_tab, x_scales)
        load_words(d_word_tab, d_words)
        nc.sync.dma_start(w_next[:], w_flat[:, W_HEAD : 2 * N])
        nc.sync.dma_start(w_third[:], w_rows[:, 2, :])
        nc.sync.dma_start(w_last[:], w_rows[:, 3, 0 : N - W_TAIL])
        load_words(x_word_tab, x_words)
        nc.sync.dma_start(w_tail[:], w_rows[:, 3, N - W_TAIL :])

        g_abs = tile([P, SLOTS], F32, "g_abs")
        g_step = tile([P, SLOTS], F32, "g_step")
        g_sign = tile([P, SLOTS], F32, "g_sign")
        nc.scalar.activation(g_step[:], g[:], ACT.Sign)
        nc.scalar.activation(g_abs[:], g[:], ACT.Abs, scale=SCORE_SCALE)
        nc.scalar.activation(g_sign[:], g_step[:], ACT.Sign, bias=0.5)

        d_scale_got = tile([P, 2 * H], U8, "d_scale_got")
        x_scale_got = tile([P, S], U8, "x_scale_got")
        dealt = tile_at(DEALT_AT, [P, 2 * H + S], U8, "dealt")

        nc.vector.tensor_copy(d_scale_got[:, 0:H], d_scale_tab[:].indirect(k1_sb[:]))
        nc.vector.tensor_copy(d_scale_got[:, H : 2 * H], d_scale_tab[:].indirect(k2_sb[:]))
        nc.vector.tensor_copy(x_scale_got[:], x_scale_tab[:].indirect(offs_sb[:]))
        nc.vector.tensor_copy(
            dealt[:, 0 : 2 * H].rearrange("p (l t m) -> p l t m", l=2, t=SLOTS),
            d_scale_got[:].rearrange("p (l m t) -> p l t m", l=2, t=SLOTS),
        )
        nc.vector.tensor_copy(dealt[:, 2 * H :].bitcast(I32), x_scale_got[:].bitcast(I32))
        for r in range(4):
            nc.sync.dma_start(planes[:].bitcast(I32)[r:P:32, :], dealt[:].bitcast(I32)[RUN * r : P : 32, :])

        w_woven = tile([P, SLOTS * N], BF16, "w_woven")
        w_signed = tile([P, SLOTS, N], BF16, "w_signed")
        parts = [
            (0, 0, w_head[:]),
            (0, W_HEAD, w_next[:, 0 : N - W_HEAD]),
            (1, 0, w_next[:, N - W_HEAD :]),
            (2, 0, w_third[:]),
            (3, 0, w_last[:]),
        ]

        def sign(t, first, rows):
            nc.scalar.activation(w_signed[:, t, first : first + rows.shape[1]], rows, ACT.Copy, scale=g_sign[:, t : t + 1])

        def weave_w(cols):
            nc.scalar.copy(
                w_woven[:].rearrange("p (m t) -> p m t", t=SLOTS)[:, cols, :], w_signed[:].rearrange("p t m -> p m t")[:, cols, :]
            )

        for part in parts:
            sign(*part)
        weave_w(slice(0, N - W_TAIL))
        sign(SLOTS - 1, N - W_TAIL, w_tail[:])
        weave_w(slice(N - W_TAIL, N))

        def deal(codes, got):
            nc.vector.tensor_copy(
                codes[:].bitcast(I32).rearrange("p (t m) -> p m t", t=SLOTS),
                got[:].bitcast(I32).rearrange("p (m t) -> p m t", t=SLOTS),
            )
            return codes

        def quantise(codes, woven, name):
            plane = tile([P, woven.shape[1] // SLOTS], U8, name)
            nc.vector.quantize_mx(out=codes[:].bitcast(FP8X4), scales=plane[:], in_=woven[:])
            return codes, plane

        def scores(h):
            banks = {}
            for pair in range(2):
                for side in range(2):
                    bank = ps.tile([P, 2, HALF], F32, name="bank_%s%d%d" % ("ab"[side], h, pair))
                    for u in range(2):
                        t = 2 * pair + u
                        nc.tensor.matmul_mx(
                            out=bank[:, u, :],
                            lhsT=key_codes[side][:, P * t : P * (t + 1)].bitcast(FP8X4),
                            lhsT_scale=planes[:, side * H + P * t : side * H + P * (t + 1)],
                            rhs=x_codes[h][:].bitcast(FP8X4),
                            rhs_scale=planes[:, 2 * H + HALF * h : 2 * H + HALF * (h + 1)],
                            start=True,
                            stop=True,
                        )
                    banks[side, pair] = bank
            return [[banks[side, t // 2][:, t % 2, :] for t in range(SLOTS)] for side in range(2)]

        def relu_out(dst, score, slots):
            for i, t in enumerate(slots):
                nc.scalar.activation(dst[:, i, :], score[t], ACT.Relu, scale=g_abs[:, t : t + 1])

        key_got = [tile([P, H], U32, "a_got"), tile([P, H], U32, "b_got")]
        for got, key_list in zip(key_got, (k1_sb, k2_sb)):
            nc.vector.tensor_copy(got[:], d_word_tab[:].indirect(key_list[:]))
        key_codes = [deal(tile([P, H], U32, "a_codes"), key_got[0])]

        def warm_up(bank_name, passes):
            warm_bank = ps.tile([WARM_ROWS, H], F32, name=bank_name)
            for i in range(passes):
                nc.tensor.matmul_mx(
                    out=warm_bank[:],
                    lhsT=key_got[0][:, 0:WARM_ROWS].bitcast(FP8X4),
                    lhsT_scale=d_scale_got[:, 0:WARM_ROWS],
                    rhs=key_got[0][:].bitcast(FP8X4),
                    rhs_scale=d_scale_got[:, 0:H],
                    start=True,
                    stop=True,
                )

        warm_up("bank_b11", 3)

        x_codes = []
        for h in range(2):
            got = tile_at(X_LAST_AT, [P, HALF], U32, "x_codes1") if h else tile([P, HALF], U32, "x_codes0")
            nc.vector.tensor_copy(got[:], x_word_tab[:].indirect(offs_sb[:, 16 * h : 16 * (h + 1)]))
            x_codes.append(got)
            if h == 0:
                key_codes.append(deal(tile_at(B_CODES_AT, [P, H], U32, "b_codes"), key_got[1]))
        w_all = quantise(tile_at(W_CODES_AT, [P, N], U32, "w_codes"), w_woven, "w_plane")
        w_mx = [[part[:, P * v : P * (v + 1)] for part in w_all] for v in range(SLOTS)]

        ra = [tile([P, SLOTS, HALF], BF16, "ra%d" % h) for h in range(2)]
        z = [tile([P, SLOTS, HALF], BF16, "z%d" % h) for h in range(2)]
        rb = tile([P, 2, HALF], BF16, "rb")

        def best(h, t, b_scores):
            nc.vector.scalar_tensor_tensor(z[h][:, t, :], b_scores[t], g_abs[:, t : t + 1], ra[h][:, t, :], ALU.mult, ALU.max)

        a_scores, b_scores = scores(0)
        relu_out(ra[0], a_scores, range(SLOTS))
        for t in range(SLOTS):
            best(0, t, b_scores)
        a_scores, b_scores = scores(1)
        relu_out(ra[1], a_scores, range(SLOTS))
        relu_out(rb, b_scores, range(2, SLOTS))
        warm_up("bank_a11", 1)
        best(1, 0, b_scores)

        out_rows = out.rearrange("(v p) j -> p v j", p=P)

        def weave_and_quantise(h):
            woven = [tile([P, QUARTER * SLOTS], BF16, "z_woven%d%d" % (h, c)) for c in range(2)]
            for c in range(2):
                nc.vector.tensor_copy(
                    woven[c][:].rearrange("p (c i t) -> p c t i", i=4, t=SLOTS),
                    z[h][:, :, QUARTER * c : QUARTER * (c + 1)].rearrange("p t (c i) -> p c t i", i=4),
                )
            return [quantise(tile([P, QUARTER], U32, "z_codes%d%d" % (h, c)), woven[c], "z_plane%d%d" % (h, c)) for c in range(2)]

        def values(h, z_mx, copies, stores):
            banks = [ps.tile([P, 2, QUARTER], F32, name="bank_%s%d%d" % ("ab"[v // 2], h, v % 2)) for v in range(SLOTS)]
            for c in range(2):
                for v in range(SLOTS):
                    nc.tensor.matmul_mx(
                        out=banks[v][:, c, :],
                        lhsT=w_mx[v][0].bitcast(FP8X4),
                        lhsT_scale=w_mx[v][1],
                        rhs=z_mx[c][0][:].bitcast(FP8X4),
                        rhs_scale=z_mx[c][1][:],
                        start=True,
                        stop=True,
                    )
            for blocks in stores:
                res = tile([P, len(blocks), HALF], F32, "res%d%d" % (h, blocks[0]))
                for u, v in enumerate(blocks):
                    copies[v](res[:, u, :], banks[v][:].rearrange("p c j -> p (c j)"))
                nc.sync.dma_start(out_rows[:, blocks[0] : blocks[-1] + 1, HALF * h : HALF * (h + 1)], res[:])

        values(0, weave_and_quantise(0), (nc.scalar.copy,) * 4, [[0, 1], [2], [3]])
        best(1, 1, b_scores)
        for c in range(2):
            cols = slice(QUARTER * c, QUARTER * (c + 1))
            nc.vector.tensor_tensor(z[1][:, 2:, cols], ra[1][:, 2:, cols], rb[:, :, cols], ALU.max)
        values(1, weave_and_quantise(1), (nc.scalar.copy, nc.vector.tensor_copy) * 2, [[0], [1], [2], [3]])
